import numpy as np
import ml_dtypes


def mxq(x, axis, fmt="e4m3"):
    dtype, down = {"e4m3": (ml_dtypes.float8_e4m3fn, 7), "e5m2": (ml_dtypes.float8_e5m2, 14)}[fmt]
    v = np.moveaxis(np.asarray(x, np.float32).astype(ml_dtypes.bfloat16).astype(np.float64), axis, -1)
    blocks = v.reshape(v.shape[:-1] + (-1, 32))
    amax = np.abs(blocks).max(-1, keepdims=True)
    byte = np.maximum(np.where(amax > 0, np.frexp(amax)[1] - 1 + 127, 0) - down, 1)
    scale = np.exp2(byte - 127.0)
    codes = (blocks / scale).astype(np.float32).astype(dtype).astype(np.float64)
    return np.moveaxis((codes * scale).reshape(v.shape), -1, axis)


WIDE = False


def mx_kscale(k):
    if not WIDE:
        return np.ones(k)
    levels = np.array([10, -10, 5, -5, 0])
    if k % 512:
        return np.exp2(np.random.permutation(np.resize(levels, k // 32))).repeat(32)
    a = np.empty((k // 512, 16))
    for p in range(k // 512):
        a[p, :8] = np.random.permutation(np.resize(levels, 8))
        for g in range(8):
            far = levels[np.abs(levels - a[p, g]) >= 10]
            a[p, g + 8] = far[np.random.randint(len(far))]
    return np.exp2(a.ravel()).repeat(32)


def f64(x):
    return np.asarray(x).astype(np.float64)


def striped(idx):
    return np.tile(idx.reshape(-1, 16).T, (8, 1)).astype(np.uint16)


def unstriped(offs):
    return offs[:16].T.reshape(-1).astype(np.int64)


E2M1 = np.array([0.0, 0.5, 1.0, 1.5, 2.0, 3.0, 4.0, 6.0, -0.0, -0.5, -1.0, -1.5, -2.0, -3.0, -4.0, -6.0])


def pack_weight(w, fmt):
    k, n = w.shape
    w = f64(np.asarray(w, np.float32).astype(ml_dtypes.bfloat16)).reshape(k // 32, 32, n)
    amax = np.abs(w).max(1)
    if fmt == "e4m3":
        byte = np.frexp(amax)[1] - 1 + 127 - 7
    else:
        mant, ex = np.frexp(amax / 6.0)
        byte = np.where(mant > 0.5, ex, ex - 1) + 127
    byte = np.clip(np.where(amax > 0, byte, 1), 1, 254)
    scaled = (w * np.exp2(127.0 - byte)[:, None, :]).reshape(k, n).astype(np.float32)
    by_word = np.ascontiguousarray(scaled.reshape(k // 512, 128, 4, n).transpose(0, 1, 3, 2))
    if fmt == "e4m3":
        words = by_word.astype(ml_dtypes.float8_e4m3fn).view(np.uint8)
    else:
        c = by_word.astype(ml_dtypes.float4_e2m1fn).view(np.uint8) & 0xF
        words = (c[..., 0::2] | (c[..., 1::2] << 4)).reshape(k // 512, 128, 2 * n)
    return np.ascontiguousarray(words), np.ascontiguousarray(byte.astype(np.uint8).reshape(k // 512, 16, n))


def unpack_weight(words, scales, fmt):
    g, _, n = scales.shape
    words = np.ascontiguousarray(words).reshape(g, 128, n, -1)
    if fmt == "e4m3":
        vals = words.view(ml_dtypes.float8_e4m3fn).astype(np.float64)
    else:
        nib = np.empty((g, 128, n, 4), np.uint8)
        nib[..., 0::2] = words & 0xF
        nib[..., 1::2] = words >> 4
        vals = E2M1[nib]
    vals = vals * np.repeat(np.exp2(scales.astype(np.float64) - 127.0), 8, axis=1)[..., None]
    return vals.transpose(0, 1, 3, 2).reshape(g * 512, n)


def gelu(v):
    return 0.5 * v * (1.0 + np.tanh(np.sqrt(2.0 / np.pi) * (v + 0.044715 * v**3)))


K, H, N, T, S = 1024, 1024, 512, 2048, 1024

def setup_inputs():
    n = np.random.standard_normal
    s = mx_kscale(K)[:, None]
    u = mx_kscale(H)[:, None]
    tab_words, tab_scales = pack_weight(n((K, T)) * s, "e4m3")
    w4_words, w4_scales = pack_weight(n((H, N)) / np.sqrt(H) / u, "e2m1")
    return {
        "tab_words": tab_words, "tab_scales": tab_scales,
        "offs": striped(np.random.permutation(T)[:S]),
        "w1": (n((K, H)) / np.sqrt(K) / s).astype(np.float32),
        "gT": n((H, T)).astype(np.float32),
        "gain": (np.exp(0.3 * n(H)) * u[:, 0]).astype(np.float32),
        "w4_words": w4_words, "w4_scales": w4_scales,
    }

def reference(tab_words, tab_scales, offs, w1, gT, gain, w4_words, w4_scales):
    v = unpack_weight(tab_words, tab_scales, "e4m3")[:, unstriped(offs)]
    g = f64(gT)[:, unstriped(offs)]
    a = mxq(f64(w1), 0, "e4m3").T @ v
    x = a - g
    h = f64(gain)[:, None] / (1.0 + x * x)
    w4 = unpack_weight(w4_words, w4_scales, "e2m1")
    return w4.T @ mxq(h, 0, "e4m3")

@@ -1,0 +1,226 @@
+from contextlib import ExitStack
+
+import concourse.mybir as mybir
+
+K, H, N, T, S = 1024, 1024, 512, 2048, 1024
+FLOPS = 2 * K * H * S + 2 * H * N * S
+
+F32 = mybir.dt.float32
+BF16 = mybir.dt.bfloat16
+I32 = mybir.dt.int32
+U32 = mybir.dt.uint32
+U16 = mybir.dt.uint16
+U8 = mybir.dt.uint8
+FP8X4 = mybir.dt.float8_e4m3fn_x4
+FP4X4 = mybir.dt.float4_e2m1fn_x4
+ACT = mybir.ActivationFunctionType
+ALU = mybir.AluOpType
+
+P = 128
+PACK = 4
+PASS = P * PACK
+BANK = 512
+GROUP = 16
+
+
+def tile_list_atom_contact_features_kernel(tc, tab_words, tab_scales, offs, w1, gT, gain, w4_words, w4_scales, out):
+    nc = tc.nc
+    with ExitStack() as ctx:
+        keep = ctx.enter_context(tc.tile_pool(name="keep", bufs=1))
+        ring = ctx.enter_context(tc.tile_pool(name="ring", bufs=3))
+        psum_a = ctx.enter_context(tc.psum_pool(name="psum_a", bufs=4))
+        psum_o = ctx.enter_context(tc.psum_pool(name="psum_o", bufs=4))
+
+        offsets = keep.tile([P, S // GROUP], U16, name="offsets")
+        nc.sync.dma_start(offsets[:], offs)
+
+        warm = keep.tile([P, 2], F32, name="warm")
+        nc.vector.memset(warm[:], 1.0)
+        nc.scalar.activation(warm[:, 1:2], warm[:, 0:1], ACT.Abs_reciprocal_sqrt)
+
+        tab_s = keep.tile([P, T], U8, name="tab_s", align_bytes=64)
+        nc.vector.memset(tab_s[:].bitcast(I32), 0)
+        w4_s = keep.tile([P, 2 * N], U8, name="w4_s", align_bytes=64)
+        nc.vector.memset(w4_s[:].bitcast(I32), 0)
+
+        tab_w = [keep.tile([P, T], I32, name=f"tab_w{a}") for a in range(2)]
+        w1_raw = [[ring.tile([P, PACK, PASS], F32, name="w1_raw") for a in range(2)] for b in range(2)]
+        ref = [[keep.tile([P, T], F32, name=f"ref{b}{t}") for t in range(PACK)] for b in range(2)]
+        w4_w = keep.tile([P, 2, N // 2], I32, name="w4_w", align_bytes=64)
+        gain_sb = keep.tile([P, 2, PACK], F32, name="gain_sb")
+        inv_gain = keep.tile([P, 2, PACK], F32, name="inv_gain")
+
+        def load_words(a):
+            nc.sync.dma_start(tab_w[a][:], tab_words[a].rearrange("p t i -> p (t i)").bitcast(I32))
+
+        def load_w1(b, a, c0, c1):
+            rows = w1[a * PASS : (a + 1) * PASS, b * PASS + c0 : b * PASS + c1]
+            nc.sync.dma_start(w1_raw[b][a][:, :, c0:c1], rows.rearrange("(p j) c -> p j c", j=PACK))
+
+        def load_ref(b, t):
+            rows = gT[b * PASS : (b + 1) * PASS, :].rearrange("(p t) n -> t p n", t=PACK)
+            nc.sync.dma_start(ref[b][t][:], rows[t])
+
+        load_words(0)
+        for q in range(4):
+            nc.scalar.dma_start(
+                tab_s[32 * q : 32 * q + 8, :].bitcast(I32),
+                tab_scales[:, 4 * q : 4 * q + 4, :].bitcast(I32),
+            )
+        nc.scalar.dma_start(gain_sb[:], gain.rearrange("(b p t) -> p b t", b=2, t=PACK))
+        load_w1(0, 0, 0, PASS)
+        load_words(1)
+        load_w1(0, 1, 0, PASS // 2)
+        load_w1(0, 1, PASS // 2, PASS)
+        for t in range(PACK):
+            load_ref(0, t)
+        load_w1(1, 0, 0, PASS)
+        load_w1(1, 1, 0, PASS)
+        load_ref(1, 0)
+        for t in range(1, PACK):
+            load_ref(1, t)
+        nc.sync.dma_start(w4_w[:], w4_words.bitcast(I32).rearrange("a p n -> p a n"))
+        for q in range(4):
+            nc.sync.dma_start(
+                w4_s[32 * q : 32 * q + 4, :].bitcast(I32).rearrange("p (a n) -> p a n", a=2),
+                w4_scales[:, 4 * q : 4 * q + 4, :].bitcast(I32).rearrange("a p n -> p a n"),
+            )
+
+        v_w = [keep.tile([P, S], U32, name=f"v_w{a}", align_bytes=64) for a in range(2)]
+        v_s = keep.tile([P, S], U8, name="v_s", align_bytes=64)
+        w1_bf = [[ring.tile([P, PACK, P, PACK], BF16, name="w1_bf", bufs=2, align_bytes=64) for a in range(2)] for b in range(2)]
+        w1_w = [[keep.tile([P, PASS], U32, name=f"w1_w{b}{a}", align_bytes=64) for a in range(2)] for b in range(2)]
+        w1_s = [[keep.tile([P, PASS], U8, name=f"w1_s{b}{a}", align_bytes=64) for a in range(2)] for b in range(2)]
+
+        def cast_w1(b, a, m0, m1):
+            dst = w1_bf[b][a][:, :, m0:m1, :].rearrange("p t m j -> p m j t")
+            src = w1_raw[b][a][:, :, PACK * m0 : PACK * m1].rearrange("p j (m t) -> p m j t", t=PACK)
+            if (b, a) != (1, 1):
+                nc.scalar.activation(dst, src, ACT.Copy)
+            else:
+                nc.vector.tensor_copy(dst, src)
+
+        def quantize_w1(b, a):
+            nc.vector.quantize_mx(
+                out=w1_w[b][a][:].bitcast(FP8X4),
+                scales=w1_s[b][a][:],
+                in_=w1_bf[b][a][:].rearrange("p t m j -> p (t m j)"),
+            )
+
+        def gather_words(a):
+            nc.vector.tensor_copy(v_w[a][:], tab_w[a][:].bitcast(U32).indirect(offsets[:]))
+
+        gather_words(0)
+        cast_w1(0, 0, 0, P)
+        nc.vector.tensor_copy(v_s[:], tab_s[:].indirect(offsets[:]))
+        nc.vector.reciprocal(inv_gain[:], gain_sb[:])
+        gather_words(1)
+        quantize_w1(0, 0)
+        cast_w1(0, 1, 0, P // 2)
+        cast_w1(0, 1, P // 2, P)
+        quantize_w1(0, 1)
+
+        def subtract(b, t, j0, j1, picked, diff):
+            n = j1 - j0
+            acc = psum_a.tile([P, BANK], F32, name="acc")
+            for a in range(2):
+                nc.tensor.matmul_mx(
+                    out=acc[:, :n],
+                    lhsT=w1_w[b][a][:, t * P : (t + 1) * P].bitcast(FP8X4),
+                    lhsT_scale=w1_s[b][a][:, t * P : (t + 1) * P],
+                    rhs=v_w[a][:, j0:j1].bitcast(FP8X4),
+                    rhs_scale=v_s[4 * a : P, j0:j1],
+                    start=(a == 0),
+                    stop=(a == 1),
+                )
+            nc.vector.tensor_tensor(diff, acc[:, :n], picked, ALU.subtract)
+
+        def planes(b, ts, j0, j1, root):
+            n = j1 - j0
+            diff = ring.tile([P, S], F32, name="diff")
+            for i, t in enumerate(ts):
+                picked = ring.tile([P, S], F32, name="picked", bufs=2)
+                nc.vector.tensor_copy(picked[:, :n], ref[b][t][:].indirect(offsets[:, j0 // GROUP : j1 // GROUP]))
+                for c0 in range(0, n, BANK):
+                    c1 = min(n, c0 + BANK)
+                    subtract(b, t, j0 + c0, j0 + c1, picked[:, c0:c1], diff[:, i * n + c0 : i * n + c1])
+            nc.scalar.activation(diff[:, : len(ts) * n], diff[:, : len(ts) * n], ACT.Square)
+            for i, t in enumerate(ts):
+                per_row = inv_gain[:, b, t : t + 1]
+                nc.scalar.activation(root[:, t, j0:j1], diff[:, i * n : (i + 1) * n], ACT.Abs_reciprocal_sqrt, bias=per_row, scale=per_row)
+
+        h_w = [keep.tile([P, S], U32, name=f"h_w{b}", align_bytes=64) for b in range(2)]
+        h_s = [keep.tile([P, S], U8, name=f"h_s{b}", align_bytes=64) for b in range(2)]
+
+        def square_and_interleave(root, j0, j1):
+            n = j1 - j0
+            h_bf = ring.tile([P, BANK, PACK], BF16, name="h_bf", bufs=2, align_bytes=64)
+            nc.scalar.activation(
+                h_bf[:, :n, :].rearrange("p (c i) t -> p c t i", i=4),
+                root[:, :, j0:j1].rearrange("p t (c i) -> p c t i", i=4),
+                ACT.Square,
+            )
+            return h_bf
+
+        def quantize_h(b, j0, j1, h_bf):
+            nc.vector.quantize_mx(
+                out=h_w[b][:, j0:j1].bitcast(FP8X4),
+                scales=h_s[b][:, j0:j1],
+                in_=h_bf[:, : j1 - j0, :].rearrange("p n t -> p (n t)"),
+            )
+
+        def mix(dst, tile_n, j0, j1):
+            for b in range(2):
+                nc.tensor.matmul_mx(
+                    out=dst,
+                    lhsT=w4_w[:, b, tile_n * (P // 2) : (tile_n + 1) * (P // 2)].bitcast(U8).bitcast(FP4X4),
+                    lhsT_scale=w4_s[:, b * N + tile_n * P : b * N + (tile_n + 1) * P],
+                    rhs=h_w[b][:, j0:j1].bitcast(FP8X4),
+                    rhs_scale=h_s[b][:, j0:j1],
+                    start=(b == 0),
+                    stop=(b == 1),
+                )
+
+        out_rows = out.rearrange("(g p) j -> p g j", p=P)
+        result = keep.tile([P, N // P, S], F32, name="result")
+
+        roots = [keep.tile([P, PACK, S], F32, name=f"root{b}") for b in range(2)]
+        planes(0, (0,), 0, BANK, roots[0])
+        planes(0, (0,), BANK, S, roots[0])
+        for t in range(1, PACK):
+            planes(0, (t,), 0, S, roots[0])
+        for a in range(2):
+            cast_w1(1, a, 0, P)
+            quantize_w1(1, a)
+        pending = [(0, half * BANK, (half + 1) * BANK, square_and_interleave(roots[0], half * BANK, (half + 1) * BANK)) for half in range(2)]
+
+        def finish(j0, j1):
+            if j1 - j0 == BANK:
+                for g in range(N // P):
+                    sums = psum_o.tile([P, BANK], F32, name="sums")
+                    mix(sums[:], g, j0, j1)
+                    nc.scalar.copy(result[:, g, j0:j1], sums[:])
+                nc.sync.dma_start(out_rows[:, :, j0:j1], result[:, :, j0:j1])
+            else:
+                for c0 in range(j0, j1, P):
+                    sums = psum_o.tile([P, N // P, P], F32, name="sums")
+                    for g in range(N // P):
+                        mix(sums[:, g, :], g, c0, c0 + P)
+                    if j1 == S and c0 == j0:
+                        nc.vector.tensor_copy(result[:, :, c0 : c0 + P], sums[:])
+                    else:
+                        nc.scalar.copy(result[:, :, c0 : c0 + P], sums[:])
+                    nc.sync.dma_start(out_rows[:, :, c0 : c0 + P], result[:, :, c0 : c0 + P])
+
+        for j0, j1, groups in ((0, 512, ((0, 1), (2, 3))), (512, 768, ((0, 1), (2, 3))), (768, 1024, ((0, 1), (2,), (3,)))):
+            for ts in groups:
+                planes(1, ts, j0, j1, roots[1])
+                if pending:
+                    job = pending.pop(0)
+                    quantize_h(*job)
+                    if job[0] == 1:
+                        finish(job[1], job[2])
+            pending.append((1, j0, j1, square_and_interleave(roots[1], j0, j1)))
+        job = pending.pop(0)
+        quantize_h(*job)
+        finish(job[1], job[2])

@@ -39,9 +39,9 @@ def tile_list_atom_contact_features_kernel(tc, tab_words, tab_scales, offs, w1, 
         nc.scalar.activation(warm[:, 1:2], warm[:, 0:1], ACT.Abs_reciprocal_sqrt)
 
         tab_s = keep.tile([P, T], U8, name="tab_s", align_bytes=64)
-        nc.vector.memset(tab_s[:].bitcast(I32), 0)
+        nc.gpsimd.memset(tab_s[:].bitcast(I32), 0)
         w4_s = keep.tile([P, 2 * N], U8, name="w4_s", align_bytes=64)
-        nc.vector.memset(w4_s[:].bitcast(I32), 0)
+        nc.gpsimd.memset(w4_s[:].bitcast(I32), 0)
 
         tab_w = [keep.tile([P, T], I32, name=f"tab_w{a}") for a in range(2)]
         w1_raw = [[ring.tile([P, PACK, PASS], F32, name="w1_raw") for a in range(2)] for b in range(2)]
@@ -120,7 +120,7 @@ def tile_list_atom_contact_features_kernel(tc, tab_words, tab_scales, offs, w1, 
         cast_w1(0, 1, P // 2, P)
         quantize_w1(0, 1)
 
-        def subtract(b, t, j0, j1, picked, diff):
+        def plane(b, t, j0, j1, root):
             n = j1 - j0
             acc = psum_a.tile([P, BANK], F32, name="acc")
             for a in range(2):
@@ -133,94 +133,116 @@ def tile_list_atom_contact_features_kernel(tc, tab_words, tab_scales, offs, w1, 
                     start=(a == 0),
                     stop=(a == 1),
                 )
-            nc.vector.tensor_tensor(diff, acc[:, :n], picked, ALU.subtract)
+            picked = ring.tile([P, BANK], F32, name="picked")
+            nc.vector.tensor_copy(picked[:, :n], ref[b][t][:].indirect(offsets[:, j0 // GROUP : j1 // GROUP]))
+            diff = ring.tile([P, BANK], F32, name="diff", bufs=5)
+            nc.vector.tensor_tensor(diff[:, :n], acc[:, :n], picked[:, :n], ALU.subtract)
+            nc.scalar.activation(diff[:, :n], diff[:, :n], ACT.Square)
+            per_row = inv_gain[:, b, t : t + 1]
+            nc.scalar.activation(root[:, t, :], diff[:, :n], ACT.Abs_reciprocal_sqrt, bias=per_row, scale=per_row)
 
-        def planes(b, ts, j0, j1, root):
-            n = j1 - j0
-            diff = ring.tile([P, S], F32, name="diff")
-            for i, t in enumerate(ts):
-                picked = ring.tile([P, S], F32, name="picked", bufs=2)
-                nc.vector.tensor_copy(picked[:, :n], ref[b][t][:].indirect(offsets[:, j0 // GROUP : j1 // GROUP]))
-                for c0 in range(0, n, BANK):
-                    c1 = min(n, c0 + BANK)
-                    subtract(b, t, j0 + c0, j0 + c1, picked[:, c0:c1], diff[:, i * n + c0 : i * n + c1])
-            nc.scalar.activation(diff[:, : len(ts) * n], diff[:, : len(ts) * n], ACT.Square)
-            for i, t in enumerate(ts):
-                per_row = inv_gain[:, b, t : t + 1]
-                nc.scalar.activation(root[:, t, j0:j1], diff[:, i * n : (i + 1) * n], ACT.Abs_reciprocal_sqrt, bias=per_row, scale=per_row)
+        h_w, h_s = {}, {}
 
-        h_w = [keep.tile([P, S], U32, name=f"h_w{b}", align_bytes=64) for b in range(2)]
-        h_s = [keep.tile([P, S], U8, name=f"h_s{b}", align_bytes=64) for b in range(2)]
-
-        def square_and_interleave(root, j0, j1):
-            n = j1 - j0
-            h_bf = ring.tile([P, BANK, PACK], BF16, name="h_bf", bufs=2, align_bytes=64)
-            nc.scalar.activation(
-                h_bf[:, :n, :].rearrange("p (c i) t -> p c t i", i=4),
-                root[:, :, j0:j1].rearrange("p t (c i) -> p c t i", i=4),
-                ACT.Square,
-            )
+        def square_and_interleave(root, c0, c1, on_vector=False):
+            h_bf = ring.tile([P, BANK, PACK], BF16, name="h_bf", align_bytes=64)
+            dst = h_bf[:, : c1 - c0, :].rearrange("p (c i) t -> p c t i", i=4)
+            src = root[:, :, c0:c1].rearrange("p t (c i) -> p c t i", i=4)
+            if on_vector:
+                nc.vector.tensor_tensor(dst, src, src, ALU.mult)
+            else:
+                nc.scalar.activation(dst, src, ACT.Square)
             return h_bf
 
         def quantize_h(b, j0, j1, h_bf):
+            words = keep.tile([P, j1 - j0], U32, name=f"h_w{b}_{j0}", align_bytes=64)
+            scales = keep.tile([P, j1 - j0], U8, name=f"h_s{b}_{j0}", align_bytes=64)
             nc.vector.quantize_mx(
-                out=h_w[b][:, j0:j1].bitcast(FP8X4),
-                scales=h_s[b][:, j0:j1],
+                out=words[:].bitcast(FP8X4),
+                scales=scales[:],
                 in_=h_bf[:, : j1 - j0, :].rearrange("p n t -> p (n t)"),
             )
+            for c0 in range(j0, j1, P):
+                h_w[b, c0] = (words, j0)
+                h_s[b, c0] = (scales, j0)
 
-        def mix(dst, tile_n, j0, j1):
+        def mix(dst, g, j0, j1):
             for b in range(2):
+                words, base = h_w[b, j0]
+                scales, base = h_s[b, j0]
                 nc.tensor.matmul_mx(
                     out=dst,
-                    lhsT=w4_w[:, b, tile_n * (P // 2) : (tile_n + 1) * (P // 2)].bitcast(U8).bitcast(FP4X4),
-                    lhsT_scale=w4_s[:, b * N + tile_n * P : b * N + (tile_n + 1) * P],
-                    rhs=h_w[b][:, j0:j1].bitcast(FP8X4),
-                    rhs_scale=h_s[b][:, j0:j1],
+                    lhsT=w4_w[:, b, g * (P // 2) : (g + 1) * (P // 2)].bitcast(U8).bitcast(FP4X4),
+                    lhsT_scale=w4_s[:, b * N + g * P : b * N + (g + 1) * P],
+                    rhs=words[:, j0 - base : j1 - base].bitcast(FP8X4),
+                    rhs_scale=scales[:, j0 - base : j1 - base],
                     start=(b == 0),
                     stop=(b == 1),
                 )
 
         out_rows = out.rearrange("(g p) j -> p g j", p=P)
-        result = keep.tile([P, N // P, S], F32, name="result")
 
-        roots = [keep.tile([P, PACK, S], F32, name=f"root{b}") for b in range(2)]
-        planes(0, (0,), 0, BANK, roots[0])
-        planes(0, (0,), BANK, S, roots[0])
-        for t in range(1, PACK):
-            planes(0, (t,), 0, S, roots[0])
-        for a in range(2):
-            cast_w1(1, a, 0, P)
-            quantize_w1(1, a)
-        pending = [(0, half * BANK, (half + 1) * BANK, square_and_interleave(roots[0], half * BANK, (half + 1) * BANK)) for half in range(2)]
+        def finish_wide(j0):
+            for g in range(N // P):
+                sums = psum_o.tile([P, BANK], F32, name="sums")
+                mix(sums[:], g, j0, j0 + BANK)
+                result = keep.tile([P, BANK], F32, name=f"wide{g}")
+                nc.scalar.copy(result[:], sums[:])
+                nc.sync.dma_start(out_rows[:, g, j0 : j0 + BANK], result[:])
 
-        def finish(j0, j1):
-            if j1 - j0 == BANK:
-                for g in range(N // P):
-                    sums = psum_o.tile([P, BANK], F32, name="sums")
-                    mix(sums[:], g, j0, j1)
-                    nc.scalar.copy(result[:, g, j0:j1], sums[:])
-                nc.sync.dma_start(out_rows[:, :, j0:j1], result[:, :, j0:j1])
+        def finish_narrow(j0, on_vector):
+            sums = psum_o.tile([P, N // P, P], F32, name="sums")
+            for g in range(N // P):
+                mix(sums[:, g, :], g, j0, j0 + P)
+            result = keep.tile([P, N // P, P], F32, name=f"narrow{j0}")
+            if on_vector:
+                nc.vector.tensor_copy(result[:], sums[:])
             else:
-                for c0 in range(j0, j1, P):
-                    sums = psum_o.tile([P, N // P, P], F32, name="sums")
-                    for g in range(N // P):
-                        mix(sums[:, g, :], g, c0, c0 + P)
-                    if j1 == S and c0 == j0:
-                        nc.vector.tensor_copy(result[:, :, c0 : c0 + P], sums[:])
-                    else:
-                        nc.scalar.copy(result[:, :, c0 : c0 + P], sums[:])
-                    nc.sync.dma_start(out_rows[:, :, c0 : c0 + P], result[:, :, c0 : c0 + P])
+                nc.scalar.copy(result[:], sums[:])
+            nc.sync.dma_start(out_rows[:, :, j0 : j0 + P], result[:])
 
-        for j0, j1, groups in ((0, 512, ((0, 1), (2, 3))), (512, 768, ((0, 1), (2, 3))), (768, 1024, ((0, 1), (2,), (3,)))):
-            for ts in groups:
-                planes(1, ts, j0, j1, roots[1])
-                if pending:
-                    job = pending.pop(0)
-                    quantize_h(*job)
-                    if job[0] == 1:
-                        finish(job[1], job[2])
-            pending.append((1, j0, j1, square_and_interleave(roots[1], j0, j1)))
-        job = pending.pop(0)
-        quantize_h(*job)
-        finish(job[1], job[2])
+        def new_root(b, j0, j1):
+            return keep.tile([P, PACK, j1 - j0], F32, name=f"root{b}_{j0}")
+
+        low, high = new_root(0, 0, BANK), new_root(0, BANK, S)
+        plane(0, 0, 0, BANK, low)
+        plane(0, 0, BANK, S, high)
+        for t in range(1, PACK):
+            plane(0, t, 0, BANK, low)
+        h_low = square_and_interleave(low, 0, BANK)
+        for t in range(1, PACK):
+            plane(0, t, BANK, S, high)
+            if t < 3:
+                cast_w1(1, t - 1, 0, P)
+            if t > 1:
+                quantize_w1(1, t - 2)
+        quantize_h(0, 0, BANK, h_low)
+        h_high = square_and_interleave(high, 0, BANK)
+
+        first = new_root(1, 0, BANK)
+        for t in range(PACK):
+            plane(1, t, 0, BANK, first)
+            if t == 1:
+                quantize_h(0, BANK, S, h_high)
+        h_first = square_and_interleave(first, 0, BANK)
+
+        second = new_root(1, 512, 768)
+        for t in range(PACK):
+            plane(1, t, 512, 768, second)
+            if t == 2:
+                quantize_h(1, 0, BANK, h_first)
+        h_second = square_and_interleave(second, 0, 256)
+        finish_wide(0)
+
+        third = new_root(1, 768, S)
+        for t in range(PACK):
+            plane(1, t, 768, S, third)
+            if t == 1:
+                quantize_h(1, 512, 768, h_second)
+        h_a = square_and_interleave(third, 0, P)
+        h_b = square_and_interleave(third, P, 2 * P, on_vector=True)
+        quantize_h(1, 768, 896, h_a)
+        quantize_h(1, 896, S, h_b)
+        finish_narrow(512, False)
+        finish_narrow(640, False)
+        finish_narrow(768, False)
+        finish_narrow(896, True)

@@ -21,6 +21,8 @@ PACK = 4
 PASS = P * PACK
 BANK = 512
 GROUP = 16
+LOADS = [('ref', 0, 0), ('ref', 0, 1), ('w1', 0), ('ref', 0, 2), ('w1', 1), ('ref', 0, 3), ('ref', 1, 0), ('ref', 1, 1), ('ref', 1, 2), ('ref', 1, 3), ('w4',)]
+STEPS = [('G', 0, 0, 0, 512), ('G', 0, 0, 512, 1024), ('D', 0, 0, 0, 512), ('D', 0, 0, 512, 1024), ('Q', 0, 0, 0, 512, 'S'), ('Q', 0, 0, 512, 1024, 'S'), ('R', 0, 0, 0, 512), ('R', 0, 0, 512, 1024), ('G', 0, 1, 0, 512), ('G', 0, 1, 512, 1024), ('D', 0, 1, 0, 512), ('D', 0, 1, 512, 1024), ('Q', 0, 1, 0, 512, 'S'), ('Q', 0, 1, 512, 1024, 'S'), ('R', 0, 1, 0, 512), ('R', 0, 1, 512, 1024), ('C', 0, 0, 128, 'S'), ('G', 0, 2, 0, 512), ('G', 0, 2, 512, 1024), ('D', 0, 2, 0, 512), ('D', 0, 2, 512, 1024), ('Q', 0, 2, 0, 512, 'V'), ('QW', 0), ('Q', 0, 2, 512, 1024, 'S'), ('R', 0, 2, 0, 512), ('R', 0, 2, 512, 1024), ('C', 1, 0, 128, 'S'), ('G', 0, 3, 0, 512), ('G', 0, 3, 512, 1024), ('D', 0, 3, 0, 512), ('D', 0, 3, 512, 1024), ('QW', 1), ('Q', 0, 3, 0, 512, 'S'), ('Q', 0, 3, 512, 1024, 'S'), ('R', 0, 3, 0, 512), ('R', 0, 3, 512, 1024), ('G', 1, 0, 0, 512), ('G', 1, 1, 0, 512), ('D', 1, 0, 0, 512), ('D', 1, 1, 0, 512), ('F', 0, 0, 0, 512, 'S'), ('QH', 0, 0, 512), ('Q', 1, 0, 0, 512, 'S'), ('Q', 1, 1, 0, 512, 'S'), ('R', 1, 0, 0, 512), ('R', 1, 1, 0, 512), ('G', 1, 2, 0, 512), ('F', 0, 512, 512, 1024, 'S'), ('G', 1, 3, 0, 512), ('D', 1, 2, 0, 512), ('D', 1, 3, 0, 512), ('Q', 1, 2, 0, 512, 'V'), ('Q', 1, 3, 0, 512, 'S'), ('R', 1, 2, 0, 512), ('R', 1, 3, 0, 512), ('G', 1, 0, 512, 768), ('G', 1, 1, 512, 768), ('QH', 0, 512, 1024), ('D', 1, 0, 512, 768), ('F', 1, 0, 0, 512, 'S'), ('D', 1, 1, 512, 768), ('Q', 1, 0, 512, 768, 'S'), ('Q', 1, 1, 512, 768, 'S'), ('R', 1, 0, 512, 768), ('R', 1, 1, 512, 768), ('G', 1, 2, 512, 768), ('G', 1, 3, 512, 768), ('D', 1, 2, 512, 768), ('QH', 1, 0, 512), ('D', 1, 3, 512, 768), ('Q', 1, 2, 512, 768, 'V'), ('Q', 1, 3, 512, 768, 'S'), ('R', 1, 2, 512, 768), ('R', 1, 3, 512, 768), ('W', 0, 0, 'S'), ('F', 1, 512, 512, 768, 'S'), ('G', 1, 0, 768, 1024), ('G', 1, 1, 768, 1024), ('D', 1, 0, 768, 1024), ('D', 1, 1, 768, 1024), ('Q', 1, 0, 768, 1024, 'S'), ('Q', 1, 1, 768, 1024, 'S'), ('R', 1, 0, 768, 1024), ('R', 1, 1, 768, 1024), ('G', 1, 2, 768, 1024), ('G', 1, 3, 768, 1024), ('D', 1, 2, 768, 1024), ('QH', 1, 512, 768), ('D', 1, 3, 768, 1024), ('W', 0, 1, 'S'), ('Q', 1, 2, 768, 1024, 'V'), ('Q', 1, 3, 768, 1024, 'S'), ('W', 0, 3, 'V'), ('R', 1, 2, 768, 1024), ('W', 0, 2, 'V'), ('R', 1, 3, 768, 1024), ('F', 1, 768, 896, 1024, 'V'), ('QH', 1, 896, 1024), ('N', 640, 'S'), ('F', 1, 768, 768, 896, 'S'), ('QH', 1, 768, 896), ('N', 512, 'S'), ('N', 896, 'V'), ('N', 768, 'S')]
 
 
 def tile_list_atom_contact_features_kernel(tc, tab_words, tab_scales, offs, w1, gT, gain, w4_words, w4_scales, out):
@@ -44,7 +46,7 @@ def tile_list_atom_contact_features_kernel(tc, tab_words, tab_scales, offs, w1, 
         nc.gpsimd.memset(w4_s[:].bitcast(I32), 0)
 
         tab_w = [keep.tile([P, T], I32, name=f"tab_w{a}") for a in range(2)]
-        w1_raw = [[ring.tile([P, PACK, PASS], F32, name="w1_raw") for a in range(2)] for b in range(2)]
+        w1_raw = [[keep.tile([P, PACK, PASS], F32, name=f"w1_raw{b}{a}") for a in range(2)] for b in range(2)]
         ref = [[keep.tile([P, T], F32, name=f"ref{b}{t}") for t in range(PACK)] for b in range(2)]
         w4_w = keep.tile([P, 2, N // 2], I32, name="w4_w", align_bytes=64)
         gain_sb = keep.tile([P, 2, PACK], F32, name="gain_sb")
@@ -63,28 +65,30 @@ def tile_list_atom_contact_features_kernel(tc, tab_words, tab_scales, offs, w1, 
 
         load_words(0)
         for q in range(4):
-            nc.scalar.dma_start(
+            nc.sync.dma_start(
                 tab_s[32 * q : 32 * q + 8, :].bitcast(I32),
                 tab_scales[:, 4 * q : 4 * q + 4, :].bitcast(I32),
             )
-        nc.scalar.dma_start(gain_sb[:], gain.rearrange("(b p t) -> p b t", b=2, t=PACK))
+        nc.sync.dma_start(gain_sb[:], gain.rearrange("(b p t) -> p b t", b=2, t=PACK))
         load_w1(0, 0, 0, PASS)
         load_words(1)
         load_w1(0, 1, 0, PASS // 2)
         load_w1(0, 1, PASS // 2, PASS)
-        for t in range(PACK):
-            load_ref(0, t)
-        load_w1(1, 0, 0, PASS)
-        load_w1(1, 1, 0, PASS)
-        load_ref(1, 0)
-        for t in range(1, PACK):
-            load_ref(1, t)
-        nc.sync.dma_start(w4_w[:], w4_words.bitcast(I32).rearrange("a p n -> p a n"))
-        for q in range(4):
-            nc.sync.dma_start(
-                w4_s[32 * q : 32 * q + 4, :].bitcast(I32).rearrange("p (a n) -> p a n", a=2),
-                w4_scales[:, 4 * q : 4 * q + 4, :].bitcast(I32).rearrange("a p n -> p a n"),
-            )
+        def load_w4():
+            nc.sync.dma_start(w4_w[:], w4_words.bitcast(I32).rearrange("a p n -> p a n"))
+            for q in range(4):
+                nc.sync.dma_start(
+                    w4_s[32 * q : 32 * q + 4, :].bitcast(I32).rearrange("p (a n) -> p a n", a=2),
+                    w4_scales[:, 4 * q : 4 * q + 4, :].bitcast(I32).rearrange("a p n -> p a n"),
+                )
+
+        for step in LOADS:
+            if step[0] == "ref":
+                load_ref(step[1], step[2])
+            elif step[0] == "w1":
+                load_w1(1, step[1], 0, PASS)
+            else:
+                load_w4()
 
         v_w = [keep.tile([P, S], U32, name=f"v_w{a}", align_bytes=64) for a in range(2)]
         v_s = keep.tile([P, S], U8, name="v_s", align_bytes=64)
@@ -92,13 +96,15 @@ def tile_list_atom_contact_features_kernel(tc, tab_words, tab_scales, offs, w1, 
         w1_w = [[keep.tile([P, PASS], U32, name=f"w1_w{b}{a}", align_bytes=64) for a in range(2)] for b in range(2)]
         w1_s = [[keep.tile([P, PASS], U8, name=f"w1_s{b}{a}", align_bytes=64) for a in range(2)] for b in range(2)]
 
-        def cast_w1(b, a, m0, m1):
+        def cast_w1(b, a, m0, m1, eng="S"):
             dst = w1_bf[b][a][:, :, m0:m1, :].rearrange("p t m j -> p m j t")
             src = w1_raw[b][a][:, :, PACK * m0 : PACK * m1].rearrange("p j (m t) -> p m j t", t=PACK)
-            if (b, a) != (1, 1):
+            if eng == "S":
                 nc.scalar.activation(dst, src, ACT.Copy)
-            else:
+            elif eng == "V":
                 nc.vector.tensor_copy(dst, src)
+            else:
+                nc.gpsimd.tensor_scalar(dst, src, 1.0, 0.0, ALU.mult, ALU.add)
 
         def quantize_w1(b, a):
             nc.vector.quantize_mx(
@@ -120,7 +126,9 @@ def tile_list_atom_contact_features_kernel(tc, tab_words, tab_scales, offs, w1, 
         cast_w1(0, 1, P // 2, P)
         quantize_w1(0, 1)
 
-        def plane(b, t, j0, j1, root):
+        accs, picks, diffs = {}, {}, {}
+
+        def gather_ref(b, t, j0, j1):
             n = j1 - j0
             acc = psum_a.tile([P, BANK], F32, name="acc")
             for a in range(2):
@@ -133,13 +141,26 @@ def tile_list_atom_contact_features_kernel(tc, tab_words, tab_scales, offs, w1, 
                     start=(a == 0),
                     stop=(a == 1),
                 )
-            picked = ring.tile([P, BANK], F32, name="picked")
+            picked = ring.tile([P, BANK], F32, name="picked", bufs=4)
             nc.vector.tensor_copy(picked[:, :n], ref[b][t][:].indirect(offsets[:, j0 // GROUP : j1 // GROUP]))
+            accs[b, t, j0], picks[b, t, j0] = acc, picked
+
+        def subtract(b, t, j0, j1):
+            n = j1 - j0
             diff = ring.tile([P, BANK], F32, name="diff", bufs=5)
-            nc.vector.tensor_tensor(diff[:, :n], acc[:, :n], picked[:, :n], ALU.subtract)
-            nc.scalar.activation(diff[:, :n], diff[:, :n], ACT.Square)
+            nc.vector.tensor_tensor(diff[:, :n], accs[b, t, j0][:, :n], picks[b, t, j0][:, :n], ALU.subtract)
+            diffs[b, t, j0] = diff[:, :n]
+
+        def square(b, t, j0, eng):
+            diff = diffs[b, t, j0]
+            if eng == "S":
+                nc.scalar.activation(diff, diff, ACT.Square)
+            else:
+                nc.vector.tensor_tensor(diff, diff, diff, ALU.mult)
+
+        def inverse_root(b, t, j0, root):
             per_row = inv_gain[:, b, t : t + 1]
-            nc.scalar.activation(root[:, t, :], diff[:, :n], ACT.Abs_reciprocal_sqrt, bias=per_row, scale=per_row)
+            nc.scalar.activation(root[:, t, :], diffs[b, t, j0], ACT.Abs_reciprocal_sqrt, bias=per_row, scale=per_row)
 
         h_w, h_s = {}, {}
 
@@ -181,12 +202,15 @@ def tile_list_atom_contact_features_kernel(tc, tab_words, tab_scales, offs, w1, 
 
         out_rows = out.rearrange("(g p) j -> p g j", p=P)
 
-        def finish_wide(j0):
-            for g in range(N // P):
+        def finish_wide(j0, groups, on_vector):
+            for g in groups:
                 sums = psum_o.tile([P, BANK], F32, name="sums")
                 mix(sums[:], g, j0, j0 + BANK)
-                result = keep.tile([P, BANK], F32, name=f"wide{g}")
-                nc.scalar.copy(result[:], sums[:])
+                result = keep.tile([P, BANK], F32, name=f"wide{g}_{j0}")
+                if on_vector:
+                    nc.vector.tensor_copy(result[:], sums[:])
+                else:
+                    nc.scalar.copy(result[:], sums[:])
                 nc.sync.dma_start(out_rows[:, g, j0 : j0 + BANK], result[:])
 
         def finish_narrow(j0, on_vector):
@@ -203,46 +227,30 @@ def tile_list_atom_contact_features_kernel(tc, tab_words, tab_scales, offs, w1, 
         def new_root(b, j0, j1):
             return keep.tile([P, PACK, j1 - j0], F32, name=f"root{b}_{j0}")
 
-        low, high = new_root(0, 0, BANK), new_root(0, BANK, S)
-        plane(0, 0, 0, BANK, low)
-        plane(0, 0, BANK, S, high)
-        for t in range(1, PACK):
-            plane(0, t, 0, BANK, low)
-        h_low = square_and_interleave(low, 0, BANK)
-        for t in range(1, PACK):
-            plane(0, t, BANK, S, high)
-            if t < 3:
-                cast_w1(1, t - 1, 0, P)
-            if t > 1:
-                quantize_w1(1, t - 2)
-        quantize_h(0, 0, BANK, h_low)
-        h_high = square_and_interleave(high, 0, BANK)
-
-        first = new_root(1, 0, BANK)
-        for t in range(PACK):
-            plane(1, t, 0, BANK, first)
-            if t == 1:
-                quantize_h(0, BANK, S, h_high)
-        h_first = square_and_interleave(first, 0, BANK)
-
-        second = new_root(1, 512, 768)
-        for t in range(PACK):
-            plane(1, t, 512, 768, second)
-            if t == 2:
-                quantize_h(1, 0, BANK, h_first)
-        h_second = square_and_interleave(second, 0, 256)
-        finish_wide(0)
-
-        third = new_root(1, 768, S)
-        for t in range(PACK):
-            plane(1, t, 768, S, third)
-            if t == 1:
-                quantize_h(1, 512, 768, h_second)
-        h_a = square_and_interleave(third, 0, P)
-        h_b = square_and_interleave(third, P, 2 * P, on_vector=True)
-        quantize_h(1, 768, 896, h_a)
-        quantize_h(1, 896, S, h_b)
-        finish_narrow(512, False)
-        finish_narrow(640, False)
-        finish_narrow(768, False)
-        finish_narrow(896, True)
+        roots, h_tiles = {}, {}
+        for step in STEPS:
+            kind = step[0]
+            if kind == "G":
+                gather_ref(*step[1:])
+            elif kind == "D":
+                subtract(*step[1:])
+            elif kind == "Q":
+                square(step[1], step[2], step[3], step[5])
+            elif kind == "R":
+                b, t, j0, j1 = step[1:]
+                if (b, j0) not in roots:
+                    roots[b, j0] = new_root(b, j0, j1)
+                inverse_root(b, t, j0, roots[b, j0])
+            elif kind == "C":
+                cast_w1(1, step[1], step[2], step[3], step[4])
+            elif kind == "QW":
+                quantize_w1(1, step[1])
+            elif kind == "F":
+                b, base, j0, j1, eng = step[1:]
+                h_tiles[b, j0] = square_and_interleave(roots[b, base], j0 - base, j1 - base, eng == "V")
+            elif kind == "QH":
+                quantize_h(step[1], step[2], step[3], h_tiles[step[1], step[2]])
+            elif kind == "W":
+                finish_wide(step[1], (step[2],), step[3] == "V")
+            else:
+                finish_narrow(step[1], step[2] == "V")

@@ -21,8 +21,6 @@ PACK = 4
 PASS = P * PACK
 BANK = 512
 GROUP = 16
-LOADS = [('ref', 0, 0), ('ref', 0, 1), ('w1', 0), ('ref', 0, 2), ('w1', 1), ('ref', 0, 3), ('ref', 1, 0), ('ref', 1, 1), ('ref', 1, 2), ('ref', 1, 3), ('w4',)]
-STEPS = [('G', 0, 0, 0, 512), ('G', 0, 0, 512, 1024), ('D', 0, 0, 0, 512), ('D', 0, 0, 512, 1024), ('Q', 0, 0, 0, 512, 'S'), ('Q', 0, 0, 512, 1024, 'S'), ('R', 0, 0, 0, 512), ('R', 0, 0, 512, 1024), ('G', 0, 1, 0, 512), ('G', 0, 1, 512, 1024), ('D', 0, 1, 0, 512), ('D', 0, 1, 512, 1024), ('Q', 0, 1, 0, 512, 'S'), ('Q', 0, 1, 512, 1024, 'S'), ('R', 0, 1, 0, 512), ('R', 0, 1, 512, 1024), ('C', 0, 0, 128, 'S'), ('G', 0, 2, 0, 512), ('G', 0, 2, 512, 1024), ('D', 0, 2, 0, 512), ('D', 0, 2, 512, 1024), ('Q', 0, 2, 0, 512, 'V'), ('QW', 0), ('Q', 0, 2, 512, 1024, 'S'), ('R', 0, 2, 0, 512), ('R', 0, 2, 512, 1024), ('C', 1, 0, 128, 'S'), ('G', 0, 3, 0, 512), ('G', 0, 3, 512, 1024), ('D', 0, 3, 0, 512), ('D', 0, 3, 512, 1024), ('QW', 1), ('Q', 0, 3, 0, 512, 'S'), ('Q', 0, 3, 512, 1024, 'S'), ('R', 0, 3, 0, 512), ('R', 0, 3, 512, 1024), ('G', 1, 0, 0, 512), ('G', 1, 1, 0, 512), ('D', 1, 0, 0, 512), ('D', 1, 1, 0, 512), ('F', 0, 0, 0, 512, 'S'), ('QH', 0, 0, 512), ('Q', 1, 0, 0, 512, 'S'), ('Q', 1, 1, 0, 512, 'S'), ('R', 1, 0, 0, 512), ('R', 1, 1, 0, 512), ('G', 1, 2, 0, 512), ('F', 0, 512, 512, 1024, 'S'), ('G', 1, 3, 0, 512), ('D', 1, 2, 0, 512), ('D', 1, 3, 0, 512), ('Q', 1, 2, 0, 512, 'V'), ('Q', 1, 3, 0, 512, 'S'), ('R', 1, 2, 0, 512), ('R', 1, 3, 0, 512), ('G', 1, 0, 512, 768), ('G', 1, 1, 512, 768), ('QH', 0, 512, 1024), ('D', 1, 0, 512, 768), ('F', 1, 0, 0, 512, 'S'), ('D', 1, 1, 512, 768), ('Q', 1, 0, 512, 768, 'S'), ('Q', 1, 1, 512, 768, 'S'), ('R', 1, 0, 512, 768), ('R', 1, 1, 512, 768), ('G', 1, 2, 512, 768), ('G', 1, 3, 512, 768), ('D', 1, 2, 512, 768), ('QH', 1, 0, 512), ('D', 1, 3, 512, 768), ('Q', 1, 2, 512, 768, 'V'), ('Q', 1, 3, 512, 768, 'S'), ('R', 1, 2, 512, 768), ('R', 1, 3, 512, 768), ('W', 0, 0, 'S'), ('F', 1, 512, 512, 768, 'S'), ('G', 1, 0, 768, 1024), ('G', 1, 1, 768, 1024), ('D', 1, 0, 768, 1024), ('D', 1, 1, 768, 1024), ('Q', 1, 0, 768, 1024, 'S'), ('Q', 1, 1, 768, 1024, 'S'), ('R', 1, 0, 768, 1024), ('R', 1, 1, 768, 1024), ('G', 1, 2, 768, 1024), ('G', 1, 3, 768, 1024), ('D', 1, 2, 768, 1024), ('QH', 1, 512, 768), ('D', 1, 3, 768, 1024), ('W', 0, 1, 'S'), ('Q', 1, 2, 768, 1024, 'V'), ('Q', 1, 3, 768, 1024, 'S'), ('W', 0, 3, 'V'), ('R', 1, 2, 768, 1024), ('W', 0, 2, 'V'), ('R', 1, 3, 768, 1024), ('F', 1, 768, 896, 1024, 'V'), ('QH', 1, 896, 1024), ('N', 640, 'S'), ('F', 1, 768, 768, 896, 'S'), ('QH', 1, 768, 896), ('N', 512, 'S'), ('N', 896, 'V'), ('N', 768, 'S')]
 
 
 def tile_list_atom_contact_features_kernel(tc, tab_words, tab_scales, offs, w1, gT, gain, w4_words, w4_scales, out):
@@ -30,20 +28,15 @@ def tile_list_atom_contact_features_kernel(tc, tab_words, tab_scales, offs, w1, 
     with ExitStack() as ctx:
         keep = ctx.enter_context(tc.tile_pool(name="keep", bufs=1))
         ring = ctx.enter_context(tc.tile_pool(name="ring", bufs=3))
-        psum_a = ctx.enter_context(tc.psum_pool(name="psum_a", bufs=4))
-        psum_o = ctx.enter_context(tc.psum_pool(name="psum_o", bufs=4))
+        psum = ctx.enter_context(tc.psum_pool(name="psum", bufs=4))
 
         offsets = keep.tile([P, S // GROUP], U16, name="offsets")
         nc.sync.dma_start(offsets[:], offs)
 
-        warm = keep.tile([P, 2], F32, name="warm")
-        nc.vector.memset(warm[:], 1.0)
-        nc.scalar.activation(warm[:, 1:2], warm[:, 0:1], ACT.Abs_reciprocal_sqrt)
-
         tab_s = keep.tile([P, T], U8, name="tab_s", align_bytes=64)
-        nc.gpsimd.memset(tab_s[:].bitcast(I32), 0)
+        nc.vector.memset(tab_s[:].bitcast(I32), 0)
         w4_s = keep.tile([P, 2 * N], U8, name="w4_s", align_bytes=64)
-        nc.gpsimd.memset(w4_s[:].bitcast(I32), 0)
+        nc.vector.memset(w4_s[:].bitcast(I32), 0)
 
         tab_w = [keep.tile([P, T], I32, name=f"tab_w{a}") for a in range(2)]
         w1_raw = [[keep.tile([P, PACK, PASS], F32, name=f"w1_raw{b}{a}") for a in range(2)] for b in range(2)]
@@ -74,21 +67,20 @@ def tile_list_atom_contact_features_kernel(tc, tab_words, tab_scales, offs, w1, 
         load_words(1)
         load_w1(0, 1, 0, PASS // 2)
         load_w1(0, 1, PASS // 2, PASS)
-        def load_w4():
-            nc.sync.dma_start(w4_w[:], w4_words.bitcast(I32).rearrange("a p n -> p a n"))
-            for q in range(4):
-                nc.sync.dma_start(
-                    w4_s[32 * q : 32 * q + 4, :].bitcast(I32).rearrange("p (a n) -> p a n", a=2),
-                    w4_scales[:, 4 * q : 4 * q + 4, :].bitcast(I32).rearrange("a p n -> p a n"),
-                )
-
-        for step in LOADS:
-            if step[0] == "ref":
-                load_ref(step[1], step[2])
-            elif step[0] == "w1":
-                load_w1(1, step[1], 0, PASS)
-            else:
-                load_w4()
+        load_ref(0, 0)
+        load_ref(0, 1)
+        load_w1(1, 0, 0, PASS)
+        load_ref(0, 2)
+        load_w1(1, 1, 0, PASS)
+        load_ref(0, 3)
+        for t in range(PACK):
+            load_ref(1, t)
+        nc.sync.dma_start(w4_w[:], w4_words.bitcast(I32).rearrange("a p n -> p a n"))
+        for q in range(4):
+            nc.sync.dma_start(
+                w4_s[32 * q : 32 * q + 4, :].bitcast(I32).rearrange("p (a n) -> p a n", a=2),
+                w4_scales[:, 4 * q : 4 * q + 4, :].bitcast(I32).rearrange("a p n -> p a n"),
+            )
 
         v_w = [keep.tile([P, S], U32, name=f"v_w{a}", align_bytes=64) for a in range(2)]
         v_s = keep.tile([P, S], U8, name="v_s", align_bytes=64)
@@ -96,73 +88,108 @@ def tile_list_atom_contact_features_kernel(tc, tab_words, tab_scales, offs, w1, 
         w1_w = [[keep.tile([P, PASS], U32, name=f"w1_w{b}{a}", align_bytes=64) for a in range(2)] for b in range(2)]
         w1_s = [[keep.tile([P, PASS], U8, name=f"w1_s{b}{a}", align_bytes=64) for a in range(2)] for b in range(2)]
 
-        def cast_w1(b, a, m0, m1, eng="S"):
+        def cast_w1(b, a, m0, m1, on_vector=False):
             dst = w1_bf[b][a][:, :, m0:m1, :].rearrange("p t m j -> p m j t")
             src = w1_raw[b][a][:, :, PACK * m0 : PACK * m1].rearrange("p j (m t) -> p m j t", t=PACK)
-            if eng == "S":
-                nc.scalar.activation(dst, src, ACT.Copy)
-            elif eng == "V":
+            if on_vector:
                 nc.vector.tensor_copy(dst, src)
             else:
-                nc.gpsimd.tensor_scalar(dst, src, 1.0, 0.0, ALU.mult, ALU.add)
+                nc.scalar.copy(dst, src)
 
-        def quantize_w1(b, a):
+        def quantize_w1(b, a, t0=0, t1=PACK):
             nc.vector.quantize_mx(
-                out=w1_w[b][a][:].bitcast(FP8X4),
-                scales=w1_s[b][a][:],
-                in_=w1_bf[b][a][:].rearrange("p t m j -> p (t m j)"),
+                out=w1_w[b][a][:, t0 * P : t1 * P].bitcast(FP8X4),
+                scales=w1_s[b][a][:, t0 * P : t1 * P],
+                in_=w1_bf[b][a][:, t0:t1].rearrange("p t m j -> p (t m j)"),
             )
 
         def gather_words(a):
             nc.vector.tensor_copy(v_w[a][:], tab_w[a][:].bitcast(U32).indirect(offsets[:]))
 
+        guess = keep.tile([P, 2, PACK], F32, name="guess")
+        mend = keep.tile([P, 2, PACK], F32, name="mend")
+        nc.scalar.activation(guess[:], gain_sb[:], ACT.Abs_reciprocal_sqrt)
+        nc.scalar.activation(guess[:], guess[:], ACT.Square)
         gather_words(0)
         cast_w1(0, 0, 0, P)
+        nc.vector.tensor_tensor(mend[:], guess[:], gain_sb[:], ALU.mult)
         nc.vector.tensor_copy(v_s[:], tab_s[:].indirect(offsets[:]))
-        nc.vector.reciprocal(inv_gain[:], gain_sb[:])
+        nc.vector.tensor_scalar(mend[:], mend[:], -1.0, 2.0, ALU.mult, ALU.add)
         gather_words(1)
+        nc.vector.tensor_tensor(inv_gain[:], guess[:], mend[:], ALU.mult)
         quantize_w1(0, 0)
         cast_w1(0, 1, 0, P // 2)
-        cast_w1(0, 1, P // 2, P)
-        quantize_w1(0, 1)
+        cast_w1(0, 1, P // 2, 3 * P // 4)
+        cast_w1(0, 1, 3 * P // 4, P, True)
+        quantize_w1(0, 1, 0, 1)
+        quantize_w1(0, 1, 1, 2)
+        quantize_w1(0, 1, 2, 4)
 
-        accs, picks, diffs = {}, {}, {}
+        def project(bank):
+            acc = psum.tile([P, BANK], F32, name="bank")
+            at = 0
+            for b, t, j0, j1 in bank:
+                for a in range(2):
+                    nc.tensor.matmul_mx(
+                        out=acc[:, at : at + j1 - j0],
+                        lhsT=w1_w[b][a][:, t * P : (t + 1) * P].bitcast(FP8X4),
+                        lhsT_scale=w1_s[b][a][:, t * P : (t + 1) * P],
+                        rhs=v_w[a][:, j0:j1].bitcast(FP8X4),
+                        rhs_scale=v_s[4 * a : P, j0:j1],
+                        start=(a == 0),
+                        stop=(a == 1),
+                    )
+                at = at + j1 - j0
+            return acc
 
-        def gather_ref(b, t, j0, j1):
-            n = j1 - j0
-            acc = psum_a.tile([P, BANK], F32, name="acc")
-            for a in range(2):
-                nc.tensor.matmul_mx(
-                    out=acc[:, :n],
-                    lhsT=w1_w[b][a][:, t * P : (t + 1) * P].bitcast(FP8X4),
-                    lhsT_scale=w1_s[b][a][:, t * P : (t + 1) * P],
-                    rhs=v_w[a][:, j0:j1].bitcast(FP8X4),
-                    rhs_scale=v_s[4 * a : P, j0:j1],
-                    start=(a == 0),
-                    stop=(a == 1),
-                )
-            picked = ring.tile([P, BANK], F32, name="picked", bufs=4)
-            nc.vector.tensor_copy(picked[:, :n], ref[b][t][:].indirect(offsets[:, j0 // GROUP : j1 // GROUP]))
-            accs[b, t, j0], picks[b, t, j0] = acc, picked
+        def latent(unit):
+            sums = ring.tile([P, 2 * BANK], F32, name="latent")
+            for i, bank in enumerate(unit):
+                nc.scalar.copy(sums[:, i * BANK : (i + 1) * BANK], project(bank)[:])
+            return sums
 
-        def subtract(b, t, j0, j1):
-            n = j1 - j0
-            diff = ring.tile([P, BANK], F32, name="diff", bufs=5)
-            nc.vector.tensor_tensor(diff[:, :n], accs[b, t, j0][:, :n], picks[b, t, j0][:, :n], ALU.subtract)
-            diffs[b, t, j0] = diff[:, :n]
+        def pieces(unit, merge):
+            found = []
+            for bank in unit:
+                for b, t, j0, j1 in bank:
+                    if merge and found and found[-1][:2] == (b, t):
+                        found[-1] = (b, t, found[-1][2], j1)
+                    else:
+                        found.append((b, t, j0, j1))
+            return found
 
-        def square(b, t, j0, eng):
-            diff = diffs[b, t, j0]
-            if eng == "S":
-                nc.scalar.activation(diff, diff, ACT.Square)
-            else:
-                nc.vector.tensor_tensor(diff, diff, diff, ALU.mult)
+        def difference(unit, sums, merge=True):
+            diff = ring.tile([P, 2 * BANK], F32, name="diff")
+            at = 0
+            for b, t, j0, j1 in pieces(unit, merge):
+                cols = slice(at, at + j1 - j0)
+                nc.vector.tensor_tensor(diff[:, cols], ref[b][t][:].indirect(offsets[:, j0 // GROUP : j1 // GROUP]), sums[:, cols], ALU.subtract)
+                at = at + j1 - j0
+            return diff
 
-        def inverse_root(b, t, j0, root):
-            per_row = inv_gain[:, b, t : t + 1]
-            nc.scalar.activation(root[:, t, :], diffs[b, t, j0], ACT.Abs_reciprocal_sqrt, bias=per_row, scale=per_row)
+        def square(diff, on_vector, parts=1):
+            for i in range(parts):
+                cols = diff[:, i * 2 * BANK // parts : (i + 1) * 2 * BANK // parts]
+                if on_vector:
+                    nc.vector.tensor_tensor(cols, cols, cols, ALU.mult)
+                else:
+                    nc.scalar.activation(cols, cols, ACT.Square)
 
-        h_w, h_s = {}, {}
+        def inverse_roots(unit, diff, chunks, merge=True):
+            at = 0
+            for b, t, j0, j1 in pieces(unit, merge):
+                per_row = inv_gain[:, b, t : t + 1]
+                for c0, c1 in chunks:
+                    lo, hi = max(c0, j0), min(c1, j1)
+                    if lo < hi:
+                        nc.scalar.activation(
+                            roots[b, c0][:, t, lo - c0 : hi - c0],
+                            diff[:, at + lo - j0 : at + hi - j0],
+                            ACT.Abs_reciprocal_sqrt,
+                            bias=per_row,
+                            scale=per_row,
+                        )
+                at = at + j1 - j0
 
         def square_and_interleave(root, c0, c1, on_vector=False):
             h_bf = ring.tile([P, BANK, PACK], BF16, name="h_bf", align_bytes=64)
@@ -174,6 +201,8 @@ def tile_list_atom_contact_features_kernel(tc, tab_words, tab_scales, offs, w1, 
                 nc.scalar.activation(dst, src, ACT.Square)
             return h_bf
 
+        h_q = {}
+
         def quantize_h(b, j0, j1, h_bf):
             words = keep.tile([P, j1 - j0], U32, name=f"h_w{b}_{j0}", align_bytes=64)
             scales = keep.tile([P, j1 - j0], U8, name=f"h_s{b}_{j0}", align_bytes=64)
@@ -183,74 +212,112 @@ def tile_list_atom_contact_features_kernel(tc, tab_words, tab_scales, offs, w1, 
                 in_=h_bf[:, : j1 - j0, :].rearrange("p n t -> p (n t)"),
             )
             for c0 in range(j0, j1, P):
-                h_w[b, c0] = (words, j0)
-                h_s[b, c0] = (scales, j0)
-
-        def mix(dst, g, j0, j1):
-            for b in range(2):
-                words, base = h_w[b, j0]
-                scales, base = h_s[b, j0]
-                nc.tensor.matmul_mx(
-                    out=dst,
-                    lhsT=w4_w[:, b, g * (P // 2) : (g + 1) * (P // 2)].bitcast(U8).bitcast(FP4X4),
-                    lhsT_scale=w4_s[:, b * N + g * P : b * N + (g + 1) * P],
-                    rhs=words[:, j0 - base : j1 - base].bitcast(FP8X4),
-                    rhs_scale=scales[:, j0 - base : j1 - base],
-                    start=(b == 0),
-                    stop=(b == 1),
-                )
+                h_q[b, c0] = (words, scales, j0)
 
         out_rows = out.rearrange("(g p) j -> p g j", p=P)
 
-        def finish_wide(j0, groups, on_vector):
-            for g in groups:
-                sums = psum_o.tile([P, BANK], F32, name="sums")
-                mix(sums[:], g, j0, j0 + BANK)
-                result = keep.tile([P, BANK], F32, name=f"wide{g}_{j0}")
-                if on_vector:
-                    nc.vector.tensor_copy(result[:], sums[:])
-                else:
-                    nc.scalar.copy(result[:], sums[:])
-                nc.sync.dma_start(out_rows[:, g, j0 : j0 + BANK], result[:])
+        def mix(sums, b, g0, g1, j0, j1):
+            step = BANK if j1 - j0 == BANK else P
+            for g in range(g0, g1):
+                for c0 in range(j0, j1, step):
+                    words, scales, base = h_q[b, c0]
+                    nc.tensor.matmul_mx(
+                        out=sums[:, g - g0, c0 - j0 : c0 - j0 + step],
+                        lhsT=w4_w[:, b, g * (P // 2) : (g + 1) * (P // 2)].bitcast(U8).bitcast(FP4X4),
+                        lhsT_scale=w4_s[:, b * N + g * P : b * N + (g + 1) * P],
+                        rhs=words[:, c0 - base : c0 - base + step].bitcast(FP8X4),
+                        rhs_scale=scales[:, c0 - base : c0 - base + step],
+                        start=(b == 0 and g == g0 and c0 == j0),
+                        stop=(b == 1 and g == g1 - 1 and c0 + step == j1),
+                    )
 
-        def finish_narrow(j0, on_vector):
-            sums = psum_o.tile([P, N // P, P], F32, name="sums")
-            for g in range(N // P):
-                mix(sums[:, g, :], g, j0, j0 + P)
-            result = keep.tile([P, N // P, P], F32, name=f"narrow{j0}")
+        def open_sums(g0, g1, j0, j1):
+            sums = psum.tile([P, g1 - g0, j1 - j0], F32, name="wide" if j0 == 0 else "bank")
+            mix(sums, 0, g0, g1, j0, j1)
+            return sums, g0, g1, j0, j1
+
+        def finish(opened, on_vector):
+            sums, g0, g1, j0, j1 = opened
+            mix(sums, 1, g0, g1, j0, j1)
+            result = keep.tile([P, g1 - g0, j1 - j0], F32, name=f"result{g0}_{j0}")
             if on_vector:
                 nc.vector.tensor_copy(result[:], sums[:])
             else:
                 nc.scalar.copy(result[:], sums[:])
-            nc.sync.dma_start(out_rows[:, :, j0 : j0 + P], result[:])
+            nc.sync.dma_start(out_rows[:, g0:g1, j0:j1], result[:])
 
-        def new_root(b, j0, j1):
-            return keep.tile([P, PACK, j1 - j0], F32, name=f"root{b}_{j0}")
+        whole = [(0, S)]
+        chunk_a, chunk_b, chunk_c = (0, 512), (512, 768), (768, 1024)
+        chunks = [chunk_a, chunk_b, chunk_c]
+        roots = {(0, 0): keep.tile([P, PACK, S], F32, name="root0")}
+        for c0, c1 in chunks:
+            roots[1, c0] = keep.tile([P, PACK, c1 - c0], F32, name=f"root1_{c0}")
+        root0 = roots[0, 0]
 
-        roots, h_tiles = {}, {}
-        for step in STEPS:
-            kind = step[0]
-            if kind == "G":
-                gather_ref(*step[1:])
-            elif kind == "D":
-                subtract(*step[1:])
-            elif kind == "Q":
-                square(step[1], step[2], step[3], step[5])
-            elif kind == "R":
-                b, t, j0, j1 = step[1:]
-                if (b, j0) not in roots:
-                    roots[b, j0] = new_root(b, j0, j1)
-                inverse_root(b, t, j0, roots[b, j0])
-            elif kind == "C":
-                cast_w1(1, step[1], step[2], step[3], step[4])
-            elif kind == "QW":
-                quantize_w1(1, step[1])
-            elif kind == "F":
-                b, base, j0, j1, eng = step[1:]
-                h_tiles[b, j0] = square_and_interleave(roots[b, base], j0 - base, j1 - base, eng == "V")
-            elif kind == "QH":
-                quantize_h(step[1], step[2], step[3], h_tiles[step[1], step[2]])
-            elif kind == "W":
-                finish_wide(step[1], (step[2],), step[3] == "V")
-            else:
-                finish_narrow(step[1], step[2] == "V")
+        def whole_plane(b, t):
+            return [[(b, t, 0, BANK)], [(b, t, BANK, S)]]
+
+        unit = [whole_plane(0, t) for t in range(PACK)] + [whole_plane(1, 0), whole_plane(1, 1)]
+        unit.append([[(1, 2, 0, BANK)], [(1, 3, 0, BANK)]])
+        unit.append([[(1, 2, c0, c1), (1, 3, c0, c1)] for c0, c1 in (chunk_b, chunk_c)])
+
+        lat0 = latent(unit[0])
+        lat1 = latent(unit[1])
+        d0 = difference(unit[0], lat0, merge=False)
+        square(d0, False, 2)
+        inverse_roots(unit[0], d0, whole, merge=False)
+        d1 = difference(unit[1], lat1)
+        lat2 = latent(unit[2])
+        cast_w1(1, 0, 0, P, True)
+        square(d1, False)
+        lat3 = latent(unit[3])
+        inverse_roots(unit[1], d1, whole)
+        d2 = difference(unit[2], lat2)
+        quantize_w1(1, 0)
+        cast_w1(1, 1, 0, 64, True)
+        cast_w1(1, 1, 64, P, False)
+        square(d2, False)
+        quantize_w1(1, 1)
+        d3 = difference(unit[3], lat3, merge=True)
+        lat4 = latent(unit[4])
+        inverse_roots(unit[2], d2, whole)
+        square(d3, False)
+        lat5 = latent(unit[5])
+        d4 = difference(unit[4], lat4, merge=False)
+        inverse_roots(unit[3], d3, whole)
+        square(d4, True, 2)
+        d5 = difference(unit[5], lat5, merge=False)
+        h00 = square_and_interleave(root0, 0, BANK)
+        lat6 = latent(unit[6])
+        inverse_roots(unit[4], d4, chunks)
+        square(d5, True, 2)
+        quantize_h(0, 0, BANK, h00)
+        sums_a = [open_sums(g, g + 1, 0, BANK) for g in range(4)]
+        d6 = difference(unit[6], lat6)
+        lat7 = latent(unit[7])
+        square(d6, True, 2)
+        inverse_roots(unit[5], d5, chunks)
+        inverse_roots(unit[6], d6, chunks)
+        d7 = difference(unit[7], lat7)
+        square(d7, True, 2)
+        h_a = square_and_interleave(roots[1, 0], 0, BANK)
+        h01 = square_and_interleave(root0, BANK, S)
+        quantize_h(1, 0, BANK, h_a)
+        inverse_roots(unit[7], d7, chunks)
+        h_b = square_and_interleave(roots[1, 512], 0, BANK // 2)
+        h_c0 = square_and_interleave(roots[1, 768], 0, P)
+        h_c1 = square_and_interleave(roots[1, 768], P, 2 * P)
+        finish(sums_a[0], True)
+        finish(sums_a[1], True)
+        quantize_h(0, BANK, S, h01)
+        sums_b = [open_sums(g, g + 2, 512, 768) for g in (0, 2)]
+        sums_c = [open_sums(0, 4, c0, c0 + P) for c0 in (768, 896)]
+        finish(sums_a[2], True)
+        finish(sums_a[3], True)
+        quantize_h(1, 512, 768, h_b)
+        quantize_h(1, 768, 896, h_c0)
+        finish(sums_b[0], True)
+        quantize_h(1, 896, 1024, h_c1)
+        finish(sums_b[1], False)
+        finish(sums_c[0], True)
+        finish(sums_c[1], False)

@@ -21,6 +21,7 @@ PACK = 4
 PASS = P * PACK
 BANK = 512
 GROUP = 16
+RUN = 2
 
 
 def tile_list_atom_contact_features_kernel(tc, tab_words, tab_scales, offs, w1, gT, gain, w4_words, w4_scales, out):
@@ -89,12 +90,22 @@ def tile_list_atom_contact_features_kernel(tc, tab_words, tab_scales, offs, w1, 
         w1_s = [[keep.tile([P, PASS], U8, name=f"w1_s{b}{a}", align_bytes=64) for a in range(2)] for b in range(2)]
 
         def cast_w1(b, a, m0, m1, on_vector=False):
-            dst = w1_bf[b][a][:, :, m0:m1, :].rearrange("p t m j -> p m j t")
-            src = w1_raw[b][a][:, :, PACK * m0 : PACK * m1].rearrange("p j (m t) -> p m j t", t=PACK)
+            dst = w1_bf[b][a][:, :, m0:m1, :].rearrange("p (u t) m j -> p u m j t", t=RUN)
+            src = w1_raw[b][a][:, :, PACK * m0 : PACK * m1].rearrange("p j (m u t) -> p u m j t", u=PACK // RUN, t=RUN)
             if on_vector:
                 nc.vector.tensor_copy(dst, src)
             else:
                 nc.scalar.copy(dst, src)
+
+        def cast_and_quantize_w1(b, a):
+            for u in range(PACK // RUN):
+                planes = slice(u * RUN, (u + 1) * RUN)
+                nc.vector.tensor_copy(
+                    w1_bf[b][a][:, planes].rearrange("p t m j -> p m j t"),
+                    w1_raw[b][a][:].rearrange("p j (m t) -> p m j t", t=PACK)[:, :, :, planes],
+                )
+            for u in range(PACK // RUN):
+                quantize_w1(b, a, u * RUN, (u + 1) * RUN)
 
         def quantize_w1(b, a, t0=0, t1=PACK):
             nc.vector.quantize_mx(
@@ -143,7 +154,7 @@ def tile_list_atom_contact_features_kernel(tc, tab_words, tab_scales, offs, w1, 
             return acc
 
         def latent(unit):
-            sums = ring.tile([P, 2 * BANK], F32, name="latent")
+            sums = ring.tile([P, 2 * BANK], F32, name="latent", bufs=4)
             for i, bank in enumerate(unit):
                 nc.scalar.copy(sums[:, i * BANK : (i + 1) * BANK], project(bank)[:])
             return sums
@@ -158,8 +169,9 @@ def tile_list_atom_contact_features_kernel(tc, tab_words, tab_scales, offs, w1, 
                         found.append((b, t, j0, j1))
             return found
 
-        def difference(unit, sums, merge=True):
-            diff = ring.tile([P, 2 * BANK], F32, name="diff")
+        diffs = [keep.tile([P, 2 * BANK], F32, name=f"diff{i}") for i in range(2)]
+
+        def difference(unit, sums, diff, merge=True):
             at = 0
             for b, t, j0, j1 in pieces(unit, merge):
                 cols = slice(at, at + j1 - j0)
@@ -167,13 +179,13 @@ def tile_list_atom_contact_features_kernel(tc, tab_words, tab_scales, offs, w1, 
                 at = at + j1 - j0
             return diff
 
-        def square(diff, on_vector, parts=1):
+        def square(dst, diff, on_vector, parts=1):
             for i in range(parts):
-                cols = diff[:, i * 2 * BANK // parts : (i + 1) * 2 * BANK // parts]
+                cols = slice(i * 2 * BANK // parts, (i + 1) * 2 * BANK // parts)
                 if on_vector:
-                    nc.vector.tensor_tensor(cols, cols, cols, ALU.mult)
+                    nc.vector.tensor_tensor(dst[:, cols], diff[:, cols], diff[:, cols], ALU.mult)
                 else:
-                    nc.scalar.activation(cols, cols, ACT.Square)
+                    nc.scalar.activation(dst[:, cols], diff[:, cols], ACT.Square)
 
         def inverse_roots(unit, diff, chunks, merge=True):
             at = 0
@@ -191,14 +203,15 @@ def tile_list_atom_contact_features_kernel(tc, tab_words, tab_scales, offs, w1, 
                         )
                 at = at + j1 - j0
 
-        def square_and_interleave(root, c0, c1, on_vector=False):
+        def square_and_interleave(root, c0, split=BANK):
             h_bf = ring.tile([P, BANK, PACK], BF16, name="h_bf", align_bytes=64)
-            dst = h_bf[:, : c1 - c0, :].rearrange("p (c i) t -> p c t i", i=4)
-            src = root[:, :, c0:c1].rearrange("p t (c i) -> p c t i", i=4)
-            if on_vector:
-                nc.vector.tensor_tensor(dst, src, src, ALU.mult)
-            else:
-                nc.scalar.activation(dst, src, ACT.Square)
+            dst = h_bf[:].rearrange("p (c i) t -> p c t i", i=RUN)
+            src = root[:, :, c0 : c0 + BANK].rearrange("p t (c i) -> p c t i", i=RUN)
+            cut = split // RUN
+            if split > 0:
+                nc.scalar.activation(dst[:, :cut], src[:, :cut], ACT.Square)
+            if split < BANK:
+                nc.vector.tensor_tensor(dst[:, cut:], src[:, cut:], src[:, cut:], ALU.mult)
             return h_bf
 
         h_q = {}
@@ -247,8 +260,7 @@ def tile_list_atom_contact_features_kernel(tc, tab_words, tab_scales, offs, w1, 
             nc.sync.dma_start(out_rows[:, g0:g1, j0:j1], result[:])
 
         whole = [(0, S)]
-        chunk_a, chunk_b, chunk_c = (0, 512), (512, 768), (768, 1024)
-        chunks = [chunk_a, chunk_b, chunk_c]
+        chunks = [(0, BANK), (BANK, S)]
         roots = {(0, 0): keep.tile([P, PACK, S], F32, name="root0")}
         for c0, c1 in chunks:
             roots[1, c0] = keep.tile([P, PACK, c1 - c0], F32, name=f"root1_{c0}")
@@ -257,67 +269,57 @@ def tile_list_atom_contact_features_kernel(tc, tab_words, tab_scales, offs, w1, 
         def whole_plane(b, t):
             return [[(b, t, 0, BANK)], [(b, t, BANK, S)]]
 
-        unit = [whole_plane(0, t) for t in range(PACK)] + [whole_plane(1, 0), whole_plane(1, 1)]
-        unit.append([[(1, 2, 0, BANK)], [(1, 3, 0, BANK)]])
-        unit.append([[(1, 2, c0, c1), (1, 3, c0, c1)] for c0, c1 in (chunk_b, chunk_c)])
+        def plane_pair(t, j0):
+            return [[(1, t, j0, j0 + BANK)], [(1, t + 1, j0, j0 + BANK)]]
+
+        unit = [whole_plane(0, t) for t in range(PACK)]
+        unit.extend([whole_plane(1, t) for t in range(PACK)])
 
         lat0 = latent(unit[0])
         lat1 = latent(unit[1])
-        d0 = difference(unit[0], lat0, merge=False)
-        square(d0, False, 2)
-        inverse_roots(unit[0], d0, whole, merge=False)
-        d1 = difference(unit[1], lat1)
+        d0 = difference(unit[0], lat0, diffs[0], merge=False)
+        square(lat0, d0, False, 2)
+        inverse_roots(unit[0], lat0, whole, merge=False)
+        d1 = difference(unit[1], lat1, diffs[1])
         lat2 = latent(unit[2])
-        cast_w1(1, 0, 0, P, True)
-        square(d1, False)
+        cast_and_quantize_w1(1, 0)
+        square(lat1, d1, False)
         lat3 = latent(unit[3])
-        inverse_roots(unit[1], d1, whole)
-        d2 = difference(unit[2], lat2)
-        quantize_w1(1, 0)
-        cast_w1(1, 1, 0, 64, True)
-        cast_w1(1, 1, 64, P, False)
-        square(d2, False)
-        quantize_w1(1, 1)
-        d3 = difference(unit[3], lat3, merge=True)
+        inverse_roots(unit[1], lat1, whole)
+        d2 = difference(unit[2], lat2, diffs[0])
+        cast_and_quantize_w1(1, 1)
+        square(lat2, d2, False)
+        d3 = difference(unit[3], lat3, diffs[1], merge=True)
+        inverse_roots(unit[2], lat2, whole)
         lat4 = latent(unit[4])
-        inverse_roots(unit[2], d2, whole)
-        square(d3, False)
+        square(lat3, d3, False)
         lat5 = latent(unit[5])
-        d4 = difference(unit[4], lat4, merge=False)
-        inverse_roots(unit[3], d3, whole)
-        square(d4, True, 2)
-        d5 = difference(unit[5], lat5, merge=False)
-        h00 = square_and_interleave(root0, 0, BANK)
+        d4 = difference(unit[4], lat4, diffs[0], merge=False)
+        inverse_roots(unit[3], lat3, whole)
+        square(lat4, d4, True, 2)
+        d5 = difference(unit[5], lat5, diffs[0], merge=False)
+        h00 = square_and_interleave(root0, 0)
         lat6 = latent(unit[6])
-        inverse_roots(unit[4], d4, chunks)
-        square(d5, True, 2)
+        inverse_roots(unit[4], lat4, chunks)
+        square(lat5, d5, True, 2)
         quantize_h(0, 0, BANK, h00)
-        sums_a = [open_sums(g, g + 1, 0, BANK) for g in range(4)]
-        d6 = difference(unit[6], lat6)
+        d6 = difference(unit[6], lat6, diffs[0], merge=False)
         lat7 = latent(unit[7])
-        square(d6, True, 2)
-        inverse_roots(unit[5], d5, chunks)
-        inverse_roots(unit[6], d6, chunks)
-        d7 = difference(unit[7], lat7)
-        square(d7, True, 2)
-        h_a = square_and_interleave(roots[1, 0], 0, BANK)
-        h01 = square_and_interleave(root0, BANK, S)
-        quantize_h(1, 0, BANK, h_a)
-        inverse_roots(unit[7], d7, chunks)
-        h_b = square_and_interleave(roots[1, 512], 0, BANK // 2)
-        h_c0 = square_and_interleave(roots[1, 768], 0, P)
-        h_c1 = square_and_interleave(roots[1, 768], P, 2 * P)
-        finish(sums_a[0], True)
-        finish(sums_a[1], True)
+        sums_a = [open_sums(g, g + 1, 0, BANK) for g in range(4)]
+        square(lat6, d6, True, 2)
+        inverse_roots(unit[5], lat5, chunks)
+        d7 = difference(unit[7], lat7, diffs[0], merge=False)
+        h01 = square_and_interleave(root0, BANK)
+        inverse_roots(unit[6], lat6, chunks)
+        square(lat7, d7, True, 2)
         quantize_h(0, BANK, S, h01)
-        sums_b = [open_sums(g, g + 2, 512, 768) for g in (0, 2)]
-        sums_c = [open_sums(0, 4, c0, c0 + P) for c0 in (768, 896)]
-        finish(sums_a[2], True)
-        finish(sums_a[3], True)
-        quantize_h(1, 512, 768, h_b)
-        quantize_h(1, 768, 896, h_c0)
-        finish(sums_b[0], True)
-        quantize_h(1, 896, 1024, h_c1)
-        finish(sums_b[1], False)
-        finish(sums_c[0], True)
-        finish(sums_c[1], False)
+        sums_b = [open_sums(g, g + 1, BANK, S) for g in range(4)]
+        inverse_roots(unit[7], lat7, chunks)
+        h_a = square_and_interleave(roots[1, 0], 0, 256)
+        quantize_h(1, 0, BANK, h_a)
+        h_b = square_and_interleave(roots[1, BANK], 0, 384)
+        for g in range(4):
+            finish(sums_a[g], g % 2 == 0)
+        quantize_h(1, BANK, S, h_b)
+        for g in range(4):
+            finish(sums_b[g], g % 2 == 0)

@@ -265,61 +265,34 @@ def tile_list_atom_contact_features_kernel(tc, tab_words, tab_scales, offs, w1, 
         for c0, c1 in chunks:
             roots[1, c0] = keep.tile([P, PACK, c1 - c0], F32, name=f"root1_{c0}")
         root0 = roots[0, 0]
+        unit = [[[(b, t, 0, BANK)], [(b, t, BANK, S)]] for b in range(2) for t in range(PACK)]
+        last = len(unit) - 1
 
-        def whole_plane(b, t):
-            return [[(b, t, 0, BANK)], [(b, t, BANK, S)]]
-
-        def plane_pair(t, j0):
-            return [[(1, t, j0, j0 + BANK)], [(1, t + 1, j0, j0 + BANK)]]
-
-        unit = [whole_plane(0, t) for t in range(PACK)]
-        unit.extend([whole_plane(1, t) for t in range(PACK)])
-
-        lat0 = latent(unit[0])
-        lat1 = latent(unit[1])
-        d0 = difference(unit[0], lat0, diffs[0], merge=False)
-        square(lat0, d0, False, 2)
-        inverse_roots(unit[0], lat0, whole, merge=False)
-        d1 = difference(unit[1], lat1, diffs[1])
-        lat2 = latent(unit[2])
-        cast_and_quantize_w1(1, 0)
-        square(lat1, d1, False)
-        lat3 = latent(unit[3])
-        inverse_roots(unit[1], lat1, whole)
-        d2 = difference(unit[2], lat2, diffs[0])
-        cast_and_quantize_w1(1, 1)
-        square(lat2, d2, False)
-        d3 = difference(unit[3], lat3, diffs[1], merge=True)
-        inverse_roots(unit[2], lat2, whole)
-        lat4 = latent(unit[4])
-        square(lat3, d3, False)
-        lat5 = latent(unit[5])
-        d4 = difference(unit[4], lat4, diffs[0], merge=False)
-        inverse_roots(unit[3], lat3, whole)
-        square(lat4, d4, True, 2)
-        d5 = difference(unit[5], lat5, diffs[0], merge=False)
-        h00 = square_and_interleave(root0, 0)
-        lat6 = latent(unit[6])
-        inverse_roots(unit[4], lat4, chunks)
-        square(lat5, d5, True, 2)
-        quantize_h(0, 0, BANK, h00)
-        d6 = difference(unit[6], lat6, diffs[0], merge=False)
-        lat7 = latent(unit[7])
-        sums_a = [open_sums(g, g + 1, 0, BANK) for g in range(4)]
-        square(lat6, d6, True, 2)
-        inverse_roots(unit[5], lat5, chunks)
-        d7 = difference(unit[7], lat7, diffs[0], merge=False)
-        h01 = square_and_interleave(root0, BANK)
-        inverse_roots(unit[6], lat6, chunks)
-        square(lat7, d7, True, 2)
-        quantize_h(0, BANK, S, h01)
-        sums_b = [open_sums(g, g + 1, BANK, S) for g in range(4)]
-        inverse_roots(unit[7], lat7, chunks)
+        lat = {u: latent(unit[u]) for u in range(2)}
+        opened, h_first = {}, {}
+        for u in range(len(unit)):
+            on_vector = u in (5, 6, 7)
+            halves = u == 0 or on_vector
+            diff = difference(unit[u], lat[u], diffs[u % 2 if u <= PACK else 1], merge=not halves)
+            if u in (1, 2):
+                cast_and_quantize_w1(1, u - 1)
+            if u in (5, 7):
+                j0 = 0 if u == 5 else BANK
+                h_first[j0] = square_and_interleave(root0, j0)
+            if u > 0:
+                inverse_roots(unit[u - 1], lat[u - 1], whole if u <= PACK else chunks, merge=u > 1)
+            if u + 2 <= last:
+                lat[u + 2] = latent(unit[u + 2])
+            square(lat[u], diff, on_vector, 2 if halves else 1)
+            if u in (5, 7):
+                quantize_h(0, j0, j0 + BANK, h_first[j0])
+                opened[j0] = [open_sums(g, g + 1, j0, j0 + BANK) for g in range(N // P)]
+        inverse_roots(unit[last], lat[last], chunks)
         h_a = square_and_interleave(roots[1, 0], 0, 256)
         quantize_h(1, 0, BANK, h_a)
         h_b = square_and_interleave(roots[1, BANK], 0, 384)
-        for g in range(4):
-            finish(sums_a[g], g % 2 == 0)
+        for g in range(N // P):
+            finish(opened[0][g], g % 2 == 0)
         quantize_h(1, BANK, S, h_b)
-        for g in range(4):
-            finish(sums_b[g], g % 2 == 0)
+        for g in range(N // P):
+            finish(opened[BANK][g], g % 2 == 0)

@@ -205,9 +205,9 @@ def tile_list_atom_contact_features_kernel(tc, tab_words, tab_scales, offs, w1, 
 
         def square_and_interleave(root, c0, split=BANK):
             h_bf = ring.tile([P, BANK, PACK], BF16, name="h_bf", align_bytes=64)
-            dst = h_bf[:].rearrange("p (c i) t -> p c t i", i=RUN)
-            src = root[:, :, c0 : c0 + BANK].rearrange("p t (c i) -> p c t i", i=RUN)
-            cut = split // RUN
+            dst = h_bf[:].rearrange("p (c i) t -> p c t i", i=PACK)
+            src = root[:, :, c0 : c0 + BANK].rearrange("p t (c i) -> p c t i", i=PACK)
+            cut = split // PACK
             if split > 0:
                 nc.scalar.activation(dst[:, :cut], src[:, :cut], ACT.Square)
             if split < BANK:

@@ -65,9 +65,8 @@ def tile_list_atom_contact_features_kernel(tc, tab_words, tab_scales, offs, w1, 
             )
         nc.sync.dma_start(gain_sb[:], gain.rearrange("(b p t) -> p b t", b=2, t=PACK))
         load_w1(0, 0, 0, PASS)
+        load_w1(0, 1, 0, PASS)
         load_words(1)
-        load_w1(0, 1, 0, PASS // 2)
-        load_w1(0, 1, PASS // 2, PASS)
         load_ref(0, 0)
         load_ref(0, 1)
         load_w1(1, 0, 0, PASS)
@@ -114,27 +113,26 @@ def tile_list_atom_contact_features_kernel(tc, tab_words, tab_scales, offs, w1, 
                 in_=w1_bf[b][a][:, t0:t1].rearrange("p t m j -> p (t m j)"),
             )
 
-        def gather_words(a):
-            nc.vector.tensor_copy(v_w[a][:], tab_w[a][:].bitcast(U32).indirect(offsets[:]))
+        def gather_words(a, j0=0, j1=S):
+            nc.vector.tensor_copy(v_w[a][:, j0:j1], tab_w[a][:].bitcast(U32).indirect(offsets[:, j0 // GROUP : j1 // GROUP]))
 
         guess = keep.tile([P, 2, PACK], F32, name="guess")
         mend = keep.tile([P, 2, PACK], F32, name="mend")
         nc.scalar.activation(guess[:], gain_sb[:], ACT.Abs_reciprocal_sqrt)
         nc.scalar.activation(guess[:], guess[:], ACT.Square)
         gather_words(0)
-        cast_w1(0, 0, 0, P)
-        nc.vector.tensor_tensor(mend[:], guess[:], gain_sb[:], ALU.mult)
+        cast_w1(0, 0, 0, 96)
+        nc.gpsimd.tensor_tensor(mend[:], guess[:], gain_sb[:], ALU.mult)
         nc.vector.tensor_copy(v_s[:], tab_s[:].indirect(offsets[:]))
-        nc.vector.tensor_scalar(mend[:], mend[:], -1.0, 2.0, ALU.mult, ALU.add)
-        gather_words(1)
-        nc.vector.tensor_tensor(inv_gain[:], guess[:], mend[:], ALU.mult)
+        nc.gpsimd.tensor_scalar(mend[:], mend[:], -1.0, 2.0, ALU.mult, ALU.add)
+        cast_w1(0, 0, 96, P, True)
+        nc.gpsimd.tensor_tensor(inv_gain[:], guess[:], mend[:], ALU.mult)
         quantize_w1(0, 0)
-        cast_w1(0, 1, 0, P // 2)
-        cast_w1(0, 1, P // 2, 3 * P // 4)
-        cast_w1(0, 1, 3 * P // 4, P, True)
-        quantize_w1(0, 1, 0, 1)
-        quantize_w1(0, 1, 1, 2)
-        quantize_w1(0, 1, 2, 4)
+        cast_w1(0, 1, 0, 64)
+        cast_w1(0, 1, 64, P, True)
+        quantize_w1(0, 1)
+        for j0, j1 in ((0, 256), (256, BANK), (BANK, S)):
+            gather_words(1, j0, j1)
 
         def project(bank):
             acc = psum.tile([P, BANK], F32, name="bank")
@@ -155,8 +153,9 @@ def tile_list_atom_contact_features_kernel(tc, tab_words, tab_scales, offs, w1, 
 
         def latent(unit):
             sums = ring.tile([P, 2 * BANK], F32, name="latent", bufs=4)
-            for i, bank in enumerate(unit):
-                nc.scalar.copy(sums[:, i * BANK : (i + 1) * BANK], project(bank)[:])
+            for bank in unit:
+                j0, j1 = bank[0][2], bank[-1][3]
+                nc.scalar.copy(sums[:, j0:j1], project(bank)[:, : j1 - j0])
             return sums
 
         def pieces(unit, merge):
@@ -267,6 +266,7 @@ def tile_list_atom_contact_features_kernel(tc, tab_words, tab_scales, offs, w1, 
         root0 = roots[0, 0]
         unit = [[[(b, t, 0, BANK)], [(b, t, BANK, S)]] for b in range(2) for t in range(PACK)]
         last = len(unit) - 1
+        unit[0] = [[(0, 0, 0, 256)], [(0, 0, 256, BANK)], [(0, 0, BANK, S)]]
 
         lat = {u: latent(unit[u]) for u in range(2)}
         opened, h_first = {}, {}
@@ -280,7 +280,7 @@ def tile_list_atom_contact_features_kernel(tc, tab_words, tab_scales, offs, w1, 
                 j0 = 0 if u == 5 else BANK
                 h_first[j0] = square_and_interleave(root0, j0)
             if u > 0:
-                inverse_roots(unit[u - 1], lat[u - 1], whole if u <= PACK else chunks, merge=u > 1)
+                inverse_roots(unit[u - 1] if u > 1 else [[(0, 0, 0, BANK)], [(0, 0, BANK, S)]], lat[u - 1], whole if u <= PACK else chunks, merge=u > 1)
             if u + 2 <= last:
                 lat[u + 2] = latent(unit[u + 2])
             square(lat[u], diff, on_vector, 2 if halves else 1)

@@ -73,7 +73,7 @@ def tile_list_atom_contact_features_kernel(tc, tab_words, tab_scales, offs, w1, 
         load_ref(0, 2)
         load_w1(1, 1, 0, PASS)
         load_ref(0, 3)
-        for t in range(PACK):
+        for t in range(3):
             load_ref(1, t)
         nc.sync.dma_start(w4_w[:], w4_words.bitcast(I32).rearrange("a p n -> p a n"))
         for q in range(4):
@@ -81,6 +81,8 @@ def tile_list_atom_contact_features_kernel(tc, tab_words, tab_scales, offs, w1, 
                 w4_s[32 * q : 32 * q + 4, :].bitcast(I32).rearrange("p (a n) -> p a n", a=2),
                 w4_scales[:, 4 * q : 4 * q + 4, :].bitcast(I32).rearrange("a p n -> p a n"),
             )
+        for t in range(3, PACK):
+            load_ref(1, t)
 
         v_w = [keep.tile([P, S], U32, name=f"v_w{a}", align_bytes=64) for a in range(2)]
         v_s = keep.tile([P, S], U8, name="v_s", align_bytes=64)
@@ -151,16 +153,19 @@ def tile_list_atom_contact_features_kernel(tc, tab_words, tab_scales, offs, w1, 
                 at = at + j1 - j0
             return acc
 
-        def latent(unit):
-            sums = ring.tile([P, 2 * BANK], F32, name="latent", bufs=4)
-            for bank in unit:
-                j0, j1 = bank[0][2], bank[-1][3]
-                nc.scalar.copy(sums[:, j0:j1], project(bank)[:, : j1 - j0])
-            return sums
+        copies = [keep.tile([P, S], F32, name=f"latent{i}", align_bytes=64) for i in range(3)]
+        diffs = [keep.tile([P, S], F32, name=f"diff{i}") for i in range(3)]
 
-        def pieces(unit, merge):
+        def latent(u):
+            at = 0
+            for bank in unit[u]:
+                width = sum(j1 - j0 for b, t, j0, j1 in bank)
+                nc.scalar.copy(copies[u % len(copies)][:, at : at + width], project(bank)[:, :width])
+                at = at + width
+
+        def pieces(u, merge):
             found = []
-            for bank in unit:
+            for bank in unit[u]:
                 for b, t, j0, j1 in bank:
                     if merge and found and found[-1][:2] == (b, t):
                         found[-1] = (b, t, found[-1][2], j1)
@@ -168,55 +173,60 @@ def tile_list_atom_contact_features_kernel(tc, tab_words, tab_scales, offs, w1, 
                         found.append((b, t, j0, j1))
             return found
 
-        diffs = [keep.tile([P, 2 * BANK], F32, name=f"diff{i}") for i in range(2)]
-
-        def difference(unit, sums, diff, merge=True):
+        def difference(u, merge):
             at = 0
-            for b, t, j0, j1 in pieces(unit, merge):
+            for b, t, j0, j1 in pieces(u, merge):
                 cols = slice(at, at + j1 - j0)
-                nc.vector.tensor_tensor(diff[:, cols], ref[b][t][:].indirect(offsets[:, j0 // GROUP : j1 // GROUP]), sums[:, cols], ALU.subtract)
+                picked = ref[b][t][:].indirect(offsets[:, j0 // GROUP : j1 // GROUP])
+                nc.vector.tensor_tensor(diffs[u % len(diffs)][:, cols], picked, copies[u % len(copies)][:, cols], ALU.subtract)
                 at = at + j1 - j0
-            return diff
 
-        def square(dst, diff, on_vector, parts=1):
+        def square(u, on_vector, parts):
+            width = sum(j1 - j0 for b, t, j0, j1 in pieces(u, True))
             for i in range(parts):
-                cols = slice(i * 2 * BANK // parts, (i + 1) * 2 * BANK // parts)
+                part = diffs[u % len(diffs)][:, i * width // parts : (i + 1) * width // parts]
                 if on_vector:
-                    nc.vector.tensor_tensor(dst[:, cols], diff[:, cols], diff[:, cols], ALU.mult)
+                    nc.vector.tensor_tensor(part, part, part, ALU.mult)
                 else:
-                    nc.scalar.activation(dst[:, cols], diff[:, cols], ACT.Square)
+                    nc.scalar.activation(part, part, ACT.Square)
 
-        def inverse_roots(unit, diff, chunks, merge=True):
+        def b_whole(u):
+            return u < PACK
+
+        def inverse_roots(u, parts=1, which=(0, 1)):
             at = 0
-            for b, t, j0, j1 in pieces(unit, merge):
+            for i, (b, t, j0, j1) in enumerate(pieces(u, b_whole(u))):
+                if i not in which:
+                    at = at + j1 - j0
+                    continue
                 per_row = inv_gain[:, b, t : t + 1]
-                for c0, c1 in chunks:
-                    lo, hi = max(c0, j0), min(c1, j1)
-                    if lo < hi:
-                        nc.scalar.activation(
-                            roots[b, c0][:, t, lo - c0 : hi - c0],
-                            diff[:, at + lo - j0 : at + hi - j0],
-                            ACT.Abs_reciprocal_sqrt,
-                            bias=per_row,
-                            scale=per_row,
-                        )
+                for i in range(parts):
+                    lo, hi = i * (j1 - j0) // parts, (i + 1) * (j1 - j0) // parts
+                    nc.scalar.activation(
+                        roots[b, j0][:, t, lo:hi],
+                        diffs[u % len(diffs)][:, at + lo : at + hi],
+                        ACT.Abs_reciprocal_sqrt,
+                        bias=per_row,
+                        scale=per_row,
+                    )
                 at = at + j1 - j0
 
-        def square_and_interleave(root, c0, split=BANK):
-            h_bf = ring.tile([P, BANK, PACK], BF16, name="h_bf", align_bytes=64)
-            dst = h_bf[:].rearrange("p (c i) t -> p c t i", i=PACK)
-            src = root[:, :, c0 : c0 + BANK].rearrange("p t (c i) -> p c t i", i=PACK)
+        staged = [keep.tile([P, BANK, PACK], BF16, name=f"h_bf{i}", align_bytes=64) for i in range(3)]
+
+        def square_and_interleave(h_bf, root, c0, width, split):
+            dst = h_bf[:, :width, :].rearrange("p (c i) t -> p c t i", i=PACK)
+            src = root[:, :, c0 : c0 + width].rearrange("p t (c i) -> p c t i", i=PACK)
             cut = split // PACK
             if split > 0:
                 nc.scalar.activation(dst[:, :cut], src[:, :cut], ACT.Square)
-            if split < BANK:
+            if split < width:
                 nc.vector.tensor_tensor(dst[:, cut:], src[:, cut:], src[:, cut:], ALU.mult)
             return h_bf
 
         h_q = {}
 
         def quantize_h(b, j0, j1, h_bf):
-            words = keep.tile([P, j1 - j0], U32, name=f"h_w{b}_{j0}", align_bytes=64)
+            words = keep.tile([P, j1 - j0], U32, name=f"latent{j0 // BANK}" if b == 0 else f"h_w{j0}", align_bytes=64)
             scales = keep.tile([P, j1 - j0], U8, name=f"h_s{b}_{j0}", align_bytes=64)
             nc.vector.quantize_mx(
                 out=words[:].bitcast(FP8X4),
@@ -258,41 +268,94 @@ def tile_list_atom_contact_features_kernel(tc, tab_words, tab_scales, offs, w1, 
                 nc.scalar.copy(result[:], sums[:])
             nc.sync.dma_start(out_rows[:, g0:g1, j0:j1], result[:])
 
-        whole = [(0, S)]
-        chunks = [(0, BANK), (BANK, S)]
         roots = {(0, 0): keep.tile([P, PACK, S], F32, name="root0")}
-        for c0, c1 in chunks:
-            roots[1, c0] = keep.tile([P, PACK, c1 - c0], F32, name=f"root1_{c0}")
-        root0 = roots[0, 0]
-        unit = [[[(b, t, 0, BANK)], [(b, t, BANK, S)]] for b in range(2) for t in range(PACK)]
-        last = len(unit) - 1
+        for c0 in (0, BANK):
+            roots[1, c0] = keep.tile([P, PACK, BANK], F32, name=f"root1_{c0}")
+        unit = [[[(b, t, 0, BANK)], [(b, t, BANK, S)]] for b in range(2) for t in range(PACK)][:6]
         unit[0] = [[(0, 0, 0, 256)], [(0, 0, 256, BANK)], [(0, 0, BANK, S)]]
+        last = len(unit) - 1
+        late = [(2, 0), (3, 0), (3, BANK), (2, BANK)]
+        late_diff = [diffs[i // 2][:, i % 2 * BANK : (i % 2 + 1) * BANK] for i in range(4)]
+        opened, h_bf, banks = {}, {}, {}
 
-        lat = {u: latent(unit[u]) for u in range(2)}
-        opened, h_first = {}, {}
+        def interleave(b, j0, split, slot):
+            h_bf[b, j0] = square_and_interleave(staged[slot], roots[b, j0 * b], j0 - j0 * b, BANK, split)
+
+        def quantize(b, j0):
+            quantize_h(b, j0, j0 + BANK, h_bf[b, j0])
+
+        def open_chunk(j0):
+            opened[j0] = [open_sums(g, g + 1, j0, j0 + BANK) for g in range(N // P)]
+
+        def finish_chunk(j0, first, on_vector):
+            for sums, v in zip(opened[j0][first:], on_vector):
+                finish(sums, v)
+
+        def project_late(i):
+            t, j0 = late[i]
+            banks[i] = project([(1, t, j0, j0 + BANK)])
+
+        def gather_late(i):
+            t, j0 = late[i]
+            nc.vector.tensor_copy(copies[i % 2][:, :BANK], ref[1][t][:].indirect(offsets[:, j0 // GROUP : (j0 + BANK) // GROUP]))
+
+        def subtract_late(i):
+            nc.vector.tensor_tensor(late_diff[i], banks[i][:], copies[i % 2][:, :BANK], ALU.subtract)
+
+        def root_late(i, squares):
+            t, j0 = late[i]
+            per_row = inv_gain[:, 1, t : t + 1]
+            nc.scalar.activation(roots[1, j0][:, t, :], squares, ACT.Abs_reciprocal_sqrt, bias=per_row, scale=per_row)
+
+        def square_on_gpsimd(part):
+            nc.gpsimd.tensor_tensor(part, part, part, ALU.mult)
+
+        latent(0)
+        latent(1)
         for u in range(len(unit)):
-            on_vector = u in (5, 6, 7)
-            halves = u == 0 or on_vector
-            diff = difference(unit[u], lat[u], diffs[u % 2 if u <= PACK else 1], merge=not halves)
+            difference(u, merge=u > 0)
             if u in (1, 2):
                 cast_and_quantize_w1(1, u - 1)
-            if u in (5, 7):
-                j0 = 0 if u == 5 else BANK
-                h_first[j0] = square_and_interleave(root0, j0)
             if u > 0:
-                inverse_roots(unit[u - 1] if u > 1 else [[(0, 0, 0, BANK)], [(0, 0, BANK, S)]], lat[u - 1], whole if u <= PACK else chunks, merge=u > 1)
+                inverse_roots(u - 1, 2 if u == 1 else 1)
+            if u == last:
+                interleave(0, 0, BANK, 0)
             if u + 2 <= last:
-                lat[u + 2] = latent(unit[u + 2])
-            square(lat[u], diff, on_vector, 2 if halves else 1)
-            if u in (5, 7):
-                quantize_h(0, j0, j0 + BANK, h_first[j0])
-                opened[j0] = [open_sums(g, g + 1, j0, j0 + BANK) for g in range(N // P)]
-        inverse_roots(unit[last], lat[last], chunks)
-        h_a = square_and_interleave(roots[1, 0], 0, 256)
-        quantize_h(1, 0, BANK, h_a)
-        h_b = square_and_interleave(roots[1, BANK], 0, 384)
-        for g in range(N // P):
-            finish(opened[0][g], g % 2 == 0)
-        quantize_h(1, BANK, S, h_b)
-        for g in range(N // P):
-            finish(opened[BANK][g], g % 2 == 0)
+                latent(u + 2)
+            else:
+                project_late(2 * (u + 1 - last))
+                project_late(2 * (u + 1 - last) + 1)
+            if u < last:
+                square(u, False, 2 if u == 0 else 1)
+        spare = diffs[last % len(diffs)]
+        square_on_gpsimd(spare[:, :BANK])
+        square_on_gpsimd(spare[:, BANK:])
+        gather_late(0)
+        subtract_late(0)
+        square_on_gpsimd(late_diff[0])
+        inverse_roots(last)
+        interleave(0, BANK, BANK, 1)
+        gather_late(1)
+        subtract_late(1)
+        gather_late(2)
+        subtract_late(2)
+        quantize(0, 0)
+        open_chunk(0)
+        square_on_gpsimd(late_diff[2])
+        gather_late(3)
+        subtract_late(3)
+        quantize(0, BANK)
+        open_chunk(BANK)
+        nc.scalar.activation(spare[:, BANK:], late_diff[1], ACT.Square)
+        root_late(0, late_diff[0])
+        root_late(1, spare[:, BANK:])
+        interleave(1, 0, 384, 2)
+        quantize(1, 0)
+        root_late(2, late_diff[2])
+        nc.vector.tensor_tensor(late_diff[3], late_diff[3], late_diff[3], ALU.mult)
+        root_late(3, late_diff[3])
+        finish_chunk(0, 0, (True,))
+        interleave(1, BANK, 384, 0)
+        quantize(1, BANK)
+        finish_chunk(0, len((True,)), (False, False, False))
+        finish_chunk(BANK, 0, (True, False, True, False))

@@ -22,6 +22,7 @@ PASS = P * PACK
 BANK = 512
 GROUP = 16
 RUN = 2
+HALF = 256
 
 
 def tile_list_atom_contact_features_kernel(tc, tab_words, tab_scales, offs, w1, gT, gain, w4_words, w4_scales, out):
@@ -75,7 +76,6 @@ def tile_list_atom_contact_features_kernel(tc, tab_words, tab_scales, offs, w1, 
         load_ref(0, 3)
         for t in range(3):
             load_ref(1, t)
-        nc.sync.dma_start(w4_w[:], w4_words.bitcast(I32).rearrange("a p n -> p a n"))
         for q in range(4):
             nc.sync.dma_start(
                 w4_s[32 * q : 32 * q + 4, :].bitcast(I32).rearrange("p (a n) -> p a n", a=2),
@@ -83,6 +83,7 @@ def tile_list_atom_contact_features_kernel(tc, tab_words, tab_scales, offs, w1, 
             )
         for t in range(3, PACK):
             load_ref(1, t)
+        nc.sync.dma_start(w4_w[:], w4_words.bitcast(I32).rearrange("a p n -> p a n"))
 
         v_w = [keep.tile([P, S], U32, name=f"v_w{a}", align_bytes=64) for a in range(2)]
         v_s = keep.tile([P, S], U8, name="v_s", align_bytes=64)
@@ -133,11 +134,11 @@ def tile_list_atom_contact_features_kernel(tc, tab_words, tab_scales, offs, w1, 
         cast_w1(0, 1, 0, 64)
         cast_w1(0, 1, 64, P, True)
         quantize_w1(0, 1)
-        for j0, j1 in ((0, 256), (256, BANK), (BANK, S)):
+        for j0, j1 in ((0, 256), (256, BANK), (BANK, 768), (768, S)):
             gather_words(1, j0, j1)
 
         def project(bank):
-            acc = psum.tile([P, BANK], F32, name="bank")
+            acc = psum.tile([P, BANK], F32, name="wide" if bank[0][:2] == (0, 0) else "bank")
             at = 0
             for b, t, j0, j1 in bank:
                 for a in range(2):
@@ -272,20 +273,23 @@ def tile_list_atom_contact_features_kernel(tc, tab_words, tab_scales, offs, w1, 
         for c0 in (0, BANK):
             roots[1, c0] = keep.tile([P, PACK, BANK], F32, name=f"root1_{c0}")
         unit = [[[(b, t, 0, BANK)], [(b, t, BANK, S)]] for b in range(2) for t in range(PACK)][:6]
-        unit[0] = [[(0, 0, 0, 256)], [(0, 0, 256, BANK)], [(0, 0, BANK, S)]]
+        unit[0] = [[(0, 0, j0, j0 + 256)] for j0 in range(0, S, 256)]
         last = len(unit) - 1
         late = [(2, 0), (3, 0), (3, BANK), (2, BANK)]
-        late_diff = [diffs[i // 2][:, i % 2 * BANK : (i % 2 + 1) * BANK] for i in range(4)]
+        late_tiles = [diffs[0], keep.tile([P, S], F32, name="diff_late")]
+        late_diff = [late_tiles[i // 2][:, i % 2 * BANK : (i % 2 + 1) * BANK] for i in range(4)]
         opened, h_bf, banks = {}, {}, {}
 
-        def interleave(b, j0, split, slot):
-            h_bf[b, j0] = square_and_interleave(staged[slot], roots[b, j0 * b], j0 - j0 * b, BANK, split)
+        def interleave(b, j0, split, slot, width=BANK):
+            base = j0 // BANK * BANK * b
+            h_bf[b, j0] = square_and_interleave(staged[slot], roots[b, base], j0 - base, width, split)
 
-        def quantize(b, j0):
-            quantize_h(b, j0, j0 + BANK, h_bf[b, j0])
+        def quantize(b, j0, width=BANK):
+            quantize_h(b, j0, j0 + width, h_bf[b, j0])
 
-        def open_chunk(j0):
-            opened[j0] = [open_sums(g, g + 1, j0, j0 + BANK) for g in range(N // P)]
+        def open_chunk(j0, width=BANK):
+            groups = BANK // width
+            opened[j0] = [open_sums(g, g + groups, j0, j0 + width) for g in range(0, N // P, groups)]
 
         def finish_chunk(j0, first, on_vector):
             for sums, v in zip(opened[j0][first:], on_vector):
@@ -295,17 +299,17 @@ def tile_list_atom_contact_features_kernel(tc, tab_words, tab_scales, offs, w1, 
             t, j0 = late[i]
             banks[i] = project([(1, t, j0, j0 + BANK)])
 
-        def gather_late(i):
+        def gather_late(i, c0=0, c1=BANK):
             t, j0 = late[i]
-            nc.vector.tensor_copy(copies[i % 2][:, :BANK], ref[1][t][:].indirect(offsets[:, j0 // GROUP : (j0 + BANK) // GROUP]))
+            nc.vector.tensor_copy(copies[i % 2][:, c0:c1], ref[1][t][:].indirect(offsets[:, (j0 + c0) // GROUP : (j0 + c1) // GROUP]))
 
-        def subtract_late(i):
-            nc.vector.tensor_tensor(late_diff[i], banks[i][:], copies[i % 2][:, :BANK], ALU.subtract)
+        def subtract_late(i, c0=0, c1=BANK):
+            nc.vector.tensor_tensor(late_diff[i][:, c0:c1], banks[i][:, c0:c1], copies[i % 2][:, c0:c1], ALU.subtract)
 
-        def root_late(i, squares):
+        def root_late(i, squares, c0=0, c1=BANK):
             t, j0 = late[i]
             per_row = inv_gain[:, 1, t : t + 1]
-            nc.scalar.activation(roots[1, j0][:, t, :], squares, ACT.Abs_reciprocal_sqrt, bias=per_row, scale=per_row)
+            nc.scalar.activation(roots[1, j0][:, t, c0:c1], squares[:, c0:c1], ACT.Abs_reciprocal_sqrt, bias=per_row, scale=per_row)
 
         def square_on_gpsimd(part):
             nc.gpsimd.tensor_tensor(part, part, part, ALU.mult)
@@ -337,25 +341,29 @@ def tile_list_atom_contact_features_kernel(tc, tab_words, tab_scales, offs, w1, 
         interleave(0, BANK, BANK, 1)
         gather_late(1)
         subtract_late(1)
+        nc.vector.tensor_tensor(late_diff[1], late_diff[1], late_diff[1], ALU.mult)
         gather_late(2)
         subtract_late(2)
         quantize(0, 0)
         open_chunk(0)
-        square_on_gpsimd(late_diff[2])
         gather_late(3)
         subtract_late(3)
+        nc.vector.tensor_tensor(late_diff[2], late_diff[2], late_diff[2], ALU.mult)
         quantize(0, BANK)
-        open_chunk(BANK)
-        nc.scalar.activation(spare[:, BANK:], late_diff[1], ACT.Square)
+        open_chunk(BANK, HALF)
+        open_chunk(BANK + HALF, HALF)
         root_late(0, late_diff[0])
-        root_late(1, spare[:, BANK:])
-        interleave(1, 0, 384, 2)
+        root_late(1, late_diff[1])
+        interleave(1, 0, 512, 2)
         quantize(1, 0)
         root_late(2, late_diff[2])
         nc.vector.tensor_tensor(late_diff[3], late_diff[3], late_diff[3], ALU.mult)
         root_late(3, late_diff[3])
         finish_chunk(0, 0, (True,))
-        interleave(1, BANK, 384, 0)
-        quantize(1, BANK)
+        interleave(1, BANK, 128, 0, HALF)
+        quantize(1, BANK, HALF)
+        interleave(1, BANK + HALF, 128, 1, HALF)
+        quantize(1, BANK + HALF, HALF)
         finish_chunk(0, len((True,)), (False, False, False))
-        finish_chunk(BANK, 0, (True, False, True, False))
+        finish_chunk(BANK, 0, (True, False))
+        finish_chunk(BANK + HALF, 0, (True, False))

@@ -227,7 +227,7 @@ def tile_list_atom_contact_features_kernel(tc, tab_words, tab_scales, offs, w1, 
         h_q = {}
 
         def quantize_h(b, j0, j1, h_bf):
-            words = keep.tile([P, j1 - j0], U32, name=f"latent{j0 // BANK}" if b == 0 else f"h_w{j0}", align_bytes=64)
+            words = keep.tile([P, j1 - j0], U32, name=("latent0", "h_bf0")[j0 // BANK] if b == 0 else f"h_w{j0}", align_bytes=64)
             scales = keep.tile([P, j1 - j0], U8, name=f"h_s{b}_{j0}", align_bytes=64)
             nc.vector.quantize_mx(
                 out=words[:].bitcast(FP8X4),
@@ -320,8 +320,10 @@ def tile_list_atom_contact_features_kernel(tc, tab_words, tab_scales, offs, w1, 
             difference(u, merge=u > 0)
             if u in (1, 2):
                 cast_and_quantize_w1(1, u - 1)
-            if u > 0:
-                inverse_roots(u - 1, 2 if u == 1 else 1)
+            if u == last:
+                inverse_roots(u - 1, 1, (0,))
+            elif u > 0:
+                inverse_roots(u - 1, 2 if u in (1, 4) else 1)
             if u == last:
                 interleave(0, 0, BANK, 0)
             if u + 2 <= last:
@@ -329,40 +331,45 @@ def tile_list_atom_contact_features_kernel(tc, tab_words, tab_scales, offs, w1, 
             else:
                 project_late(2 * (u + 1 - last))
                 project_late(2 * (u + 1 - last) + 1)
-            if u < last:
-                square(u, False, 2 if u == 0 else 1)
+            if u == last - 1:
+                nc.scalar.activation(diffs[u % 3][:, :BANK], diffs[u % 3][:, :BANK], ACT.Square)
+            elif u < last:
+                square(u, False, 2 if u in (0, 3) else 1)
         spare = diffs[last % len(diffs)]
+        held = diffs[(last - 1) % len(diffs)][:, BANK:]
+        nc.gpsimd.tensor_tensor(copies[2][:, BANK:], held, held, ALU.mult)
         square_on_gpsimd(spare[:, :BANK])
         square_on_gpsimd(spare[:, BANK:])
         gather_late(0)
         subtract_late(0)
         square_on_gpsimd(late_diff[0])
+        nc.scalar.activation(roots[1, BANK][:, 0, :], copies[2][:, BANK:], ACT.Abs_reciprocal_sqrt, bias=inv_gain[:, 1, 0:1], scale=inv_gain[:, 1, 0:1])
         inverse_roots(last)
         interleave(0, BANK, BANK, 1)
         gather_late(1)
         subtract_late(1)
-        nc.vector.tensor_tensor(late_diff[1], late_diff[1], late_diff[1], ALU.mult)
         gather_late(2)
         subtract_late(2)
         quantize(0, 0)
         open_chunk(0)
+        square_on_gpsimd(late_diff[2])
         gather_late(3)
         subtract_late(3)
-        nc.vector.tensor_tensor(late_diff[2], late_diff[2], late_diff[2], ALU.mult)
+        nc.scalar.activation(spare[:, BANK:], late_diff[1], ACT.Square)
+        root_late(0, late_diff[0])
+        root_late(1, spare[:, BANK:])
+        interleave(1, 0, 320, 0)
+        quantize(1, 0)
         quantize(0, BANK)
         open_chunk(BANK, HALF)
         open_chunk(BANK + HALF, HALF)
-        root_late(0, late_diff[0])
-        root_late(1, late_diff[1])
-        interleave(1, 0, 512, 2)
-        quantize(1, 0)
         root_late(2, late_diff[2])
         nc.vector.tensor_tensor(late_diff[3], late_diff[3], late_diff[3], ALU.mult)
         root_late(3, late_diff[3])
         finish_chunk(0, 0, (True,))
-        interleave(1, BANK, 128, 0, HALF)
+        interleave(1, BANK, 192, 2, HALF)
         quantize(1, BANK, HALF)
-        interleave(1, BANK + HALF, 128, 1, HALF)
+        interleave(1, BANK + HALF, 192, 1, HALF)
         quantize(1, BANK + HALF, HALF)
         finish_chunk(0, len((True,)), (False, False, False))
         finish_chunk(BANK, 0, (True, False))

from contextlib import ExitStack

import concourse.mybir as mybir

K, H, N, T, S = 1024, 1024, 512, 2048, 1024
FLOPS = 2 * K * H * S + 2 * H * N * S

F32 = mybir.dt.float32
BF16 = mybir.dt.bfloat16
I32 = mybir.dt.int32
U32 = mybir.dt.uint32
U16 = mybir.dt.uint16
U8 = mybir.dt.uint8
FP8X4 = mybir.dt.float8_e4m3fn_x4
FP4X4 = mybir.dt.float4_e2m1fn_x4
ACT = mybir.ActivationFunctionType
ALU = mybir.AluOpType

P = 128
PACK = 4
PASS = P * PACK
BANK = 512
GROUP = 16
RUN = 2
HALF = 256


def tile_list_atom_contact_features_kernel(tc, tab_words, tab_scales, offs, w1, gT, gain, w4_words, w4_scales, out):
    nc = tc.nc
    with ExitStack() as ctx:
        keep = ctx.enter_context(tc.tile_pool(name="keep", bufs=1))
        ring = ctx.enter_context(tc.tile_pool(name="ring", bufs=3))
        psum = ctx.enter_context(tc.psum_pool(name="psum", bufs=4))

        offsets = keep.tile([P, S // GROUP], U16, name="offsets")
        nc.sync.dma_start(offsets[:], offs)

        tab_s = keep.tile([P, T], U8, name="tab_s", align_bytes=64)
        nc.vector.memset(tab_s[:].bitcast(I32), 0)
        w4_s = keep.tile([P, 2 * N], U8, name="w4_s", align_bytes=64)
        nc.vector.memset(w4_s[:].bitcast(I32), 0)

        tab_w = [keep.tile([P, T], I32, name=f"tab_w{a}") for a in range(2)]
        w1_raw = [[keep.tile([P, PACK, PASS], F32, name=f"w1_raw{b}{a}") for a in range(2)] for b in range(2)]
        ref = [[keep.tile([P, T], F32, name=f"ref{b}{t}") for t in range(PACK)] for b in range(2)]
        w4_w = keep.tile([P, 2, N // 2], I32, name="w4_w", align_bytes=64)
        gain_sb = keep.tile([P, 2, PACK], F32, name="gain_sb")
        inv_gain = keep.tile([P, 2, PACK], F32, name="inv_gain")

        def load_words(a):
            nc.sync.dma_start(tab_w[a][:], tab_words[a].rearrange("p t i -> p (t i)").bitcast(I32))

        def load_w1(b, a, c0, c1):
            rows = w1[a * PASS : (a + 1) * PASS, b * PASS + c0 : b * PASS + c1]
            nc.sync.dma_start(w1_raw[b][a][:, :, c0:c1], rows.rearrange("(p j) c -> p j c", j=PACK))

        def load_ref(b, t):
            rows = gT[b * PASS : (b + 1) * PASS, :].rearrange("(p t) n -> t p n", t=PACK)
            nc.sync.dma_start(ref[b][t][:], rows[t])

        load_words(0)
        for q in range(4):
            nc.sync.dma_start(
                tab_s[32 * q : 32 * q + 8, :].bitcast(I32),
                tab_scales[:, 4 * q : 4 * q + 4, :].bitcast(I32),
            )
        nc.sync.dma_start(gain_sb[:], gain.rearrange("(b p t) -> p b t", b=2, t=PACK))
        load_w1(0, 0, 0, PASS)
        load_w1(0, 1, 0, PASS)
        load_words(1)
        load_ref(0, 0)
        load_ref(0, 1)
        load_w1(1, 0, 0, PASS)
        load_ref(0, 2)
        load_w1(1, 1, 0, PASS)
        load_ref(0, 3)
        for t in range(3):
            load_ref(1, t)
        for q in range(4):
            nc.sync.dma_start(
                w4_s[32 * q : 32 * q + 4, :].bitcast(I32).rearrange("p (a n) -> p a n", a=2),
                w4_scales[:, 4 * q : 4 * q + 4, :].bitcast(I32).rearrange("a p n -> p a n"),
            )
        for t in range(3, PACK):
            load_ref(1, t)
        nc.sync.dma_start(w4_w[:], w4_words.bitcast(I32).rearrange("a p n -> p a n"))

        v_w = [keep.tile([P, S], U32, name=f"v_w{a}", align_bytes=64) for a in range(2)]
        v_s = keep.tile([P, S], U8, name="v_s", align_bytes=64)
        w1_bf = [[ring.tile([P, PACK, P, PACK], BF16, name="w1_bf", bufs=2, align_bytes=64) for a in range(2)] for b in range(2)]
        w1_w = [[keep.tile([P, PASS], U32, name=f"w1_w{b}{a}", align_bytes=64) for a in range(2)] for b in range(2)]
        w1_s = [[keep.tile([P, PASS], U8, name=f"w1_s{b}{a}", align_bytes=64) for a in range(2)] for b in range(2)]

        def cast_w1(b, a, m0, m1, on_vector=False):
            dst = w1_bf[b][a][:, :, m0:m1, :].rearrange("p (u t) m j -> p u m j t", t=RUN)
            src = w1_raw[b][a][:, :, PACK * m0 : PACK * m1].rearrange("p j (m u t) -> p u m j t", u=PACK // RUN, t=RUN)
            if on_vector:
                nc.vector.tensor_copy(dst, src)
            else:
                nc.scalar.copy(dst, src)

        def cast_and_quantize_w1(b, a):
            for u in range(PACK // RUN):
                planes = slice(u * RUN, (u + 1) * RUN)
                nc.vector.tensor_copy(
                    w1_bf[b][a][:, planes].rearrange("p t m j -> p m j t"),
                    w1_raw[b][a][:].rearrange("p j (m t) -> p m j t", t=PACK)[:, :, :, planes],
                )
            for u in range(PACK // RUN):
                quantize_w1(b, a, u * RUN, (u + 1) * RUN)

        def quantize_w1(b, a, t0=0, t1=PACK):
            nc.vector.quantize_mx(
                out=w1_w[b][a][:, t0 * P : t1 * P].bitcast(FP8X4),
                scales=w1_s[b][a][:, t0 * P : t1 * P],
                in_=w1_bf[b][a][:, t0:t1].rearrange("p t m j -> p (t m j)"),
            )

        def gather_words(a, j0=0, j1=S):
            nc.vector.tensor_copy(v_w[a][:, j0:j1], tab_w[a][:].bitcast(U32).indirect(offsets[:, j0 // GROUP : j1 // GROUP]))

        guess = keep.tile([P, 2, PACK], F32, name="guess")
        mend = keep.tile([P, 2, PACK], F32, name="mend")
        nc.scalar.activation(guess[:], gain_sb[:], ACT.Abs_reciprocal_sqrt)
        nc.scalar.activation(guess[:], guess[:], ACT.Square)
        gather_words(0)
        cast_w1(0, 0, 0, 96)
        nc.gpsimd.tensor_tensor(mend[:], guess[:], gain_sb[:], ALU.mult)
        nc.vector.tensor_copy(v_s[:], tab_s[:].indirect(offsets[:]))
        nc.gpsimd.tensor_scalar(mend[:], mend[:], -1.0, 2.0, ALU.mult, ALU.add)
        cast_w1(0, 0, 96, P, True)
        nc.gpsimd.tensor_tensor(inv_gain[:], guess[:], mend[:], ALU.mult)
        quantize_w1(0, 0)
        cast_w1(0, 1, 0, 64)
        cast_w1(0, 1, 64, P, True)
        quantize_w1(0, 1)
        for j0, j1 in ((0, 256), (256, BANK), (BANK, 768), (768, S)):
            gather_words(1, j0, j1)

        def project(bank):
            acc = psum.tile([P, BANK], F32, name="wide" if bank[0][:2] == (0, 0) else "bank")
            at = 0
            for b, t, j0, j1 in bank:
                for a in range(2):
                    nc.tensor.matmul_mx(
                        out=acc[:, at : at + j1 - j0],
                        lhsT=w1_w[b][a][:, t * P : (t + 1) * P].bitcast(FP8X4),
                        lhsT_scale=w1_s[b][a][:, t * P : (t + 1) * P],
                        rhs=v_w[a][:, j0:j1].bitcast(FP8X4),
                        rhs_scale=v_s[4 * a : P, j0:j1],
                        start=(a == 0),
                        stop=(a == 1),
                    )
                at = at + j1 - j0
            return acc

        copies = [keep.tile([P, S], F32, name=f"latent{i}", align_bytes=64) for i in range(3)]
        diffs = [keep.tile([P, S], F32, name=f"diff{i}") for i in range(3)]

        def latent(u):
            at = 0
            for bank in unit[u]:
                width = sum(j1 - j0 for b, t, j0, j1 in bank)
                nc.scalar.copy(copies[u % len(copies)][:, at : at + width], project(bank)[:, :width])
                at = at + width

        def pieces(u, merge):
            found = []
            for bank in unit[u]:
                for b, t, j0, j1 in bank:
                    if merge and found and found[-1][:2] == (b, t):
                        found[-1] = (b, t, found[-1][2], j1)
                    else:
                        found.append((b, t, j0, j1))
            return found

        def difference(u, merge):
            at = 0
            for b, t, j0, j1 in pieces(u, merge):
                cols = slice(at, at + j1 - j0)
                picked = ref[b][t][:].indirect(offsets[:, j0 // GROUP : j1 // GROUP])
                nc.vector.tensor_tensor(diffs[u % len(diffs)][:, cols], picked, copies[u % len(copies)][:, cols], ALU.subtract)
                at = at + j1 - j0

        def square(u, on_vector, parts):
            width = sum(j1 - j0 for b, t, j0, j1 in pieces(u, True))
            for i in range(parts):
                part = diffs[u % len(diffs)][:, i * width // parts : (i + 1) * width // parts]
                if on_vector:
                    nc.vector.tensor_tensor(part, part, part, ALU.mult)
                else:
                    nc.scalar.activation(part, part, ACT.Square)

        def b_whole(u):
            return u < PACK

        def inverse_roots(u, parts=1, which=(0, 1)):
            at = 0
            for i, (b, t, j0, j1) in enumerate(pieces(u, b_whole(u))):
                if i not in which:
                    at = at + j1 - j0
                    continue
                per_row = inv_gain[:, b, t : t + 1]
                for i in range(parts):
                    lo, hi = i * (j1 - j0) // parts, (i + 1) * (j1 - j0) // parts
                    nc.scalar.activation(
                        roots[b, j0][:, t, lo:hi],
                        diffs[u % len(diffs)][:, at + lo : at + hi],
                        ACT.Abs_reciprocal_sqrt,
                        bias=per_row,
                        scale=per_row,
                    )
                at = at + j1 - j0

        staged = [keep.tile([P, BANK, PACK], BF16, name=f"h_bf{i}", align_bytes=64) for i in range(3)]

        def square_and_interleave(h_bf, root, c0, width, split):
            dst = h_bf[:, :width, :].rearrange("p (c i) t -> p c t i", i=PACK)
            src = root[:, :, c0 : c0 + width].rearrange("p t (c i) -> p c t i", i=PACK)
            cut = split // PACK
            if split > 0:
                nc.scalar.activation(dst[:, :cut], src[:, :cut], ACT.Square)
            if split < width:
                nc.vector.tensor_tensor(dst[:, cut:], src[:, cut:], src[:, cut:], ALU.mult)
            return h_bf

        h_q = {}

        def quantize_h(b, j0, j1, h_bf):
            words = keep.tile([P, j1 - j0], U32, name=("latent0", "h_bf0")[j0 // BANK] if b == 0 else f"h_w{j0}", align_bytes=64)
            scales = keep.tile([P, j1 - j0], U8, name=f"h_s{b}_{j0}", align_bytes=64)
            nc.vector.quantize_mx(
                out=words[:].bitcast(FP8X4),
                scales=scales[:],
                in_=h_bf[:, : j1 - j0, :].rearrange("p n t -> p (n t)"),
            )
            for c0 in range(j0, j1, P):
                h_q[b, c0] = (words, scales, j0)

        out_rows = out.rearrange("(g p) j -> p g j", p=P)

        def mix(sums, b, g0, g1, j0, j1):
            step = BANK if j1 - j0 == BANK else P
            for g in range(g0, g1):
                for c0 in range(j0, j1, step):
                    words, scales, base = h_q[b, c0]
                    nc.tensor.matmul_mx(
                        out=sums[:, g - g0, c0 - j0 : c0 - j0 + step],
                        lhsT=w4_w[:, b, g * (P // 2) : (g + 1) * (P // 2)].bitcast(U8).bitcast(FP4X4),
                        lhsT_scale=w4_s[:, b * N + g * P : b * N + (g + 1) * P],
                        rhs=words[:, c0 - base : c0 - base + step].bitcast(FP8X4),
                        rhs_scale=scales[:, c0 - base : c0 - base + step],
                        start=(b == 0 and g == g0 and c0 == j0),
                        stop=(b == 1 and g == g1 - 1 and c0 + step == j1),
                    )

        def open_sums(g0, g1, j0, j1):
            sums = psum.tile([P, g1 - g0, j1 - j0], F32, name="wide" if j0 == 0 else "bank")
            mix(sums, 0, g0, g1, j0, j1)
            return sums, g0, g1, j0, j1

        def finish(opened, on_vector):
            sums, g0, g1, j0, j1 = opened
            mix(sums, 1, g0, g1, j0, j1)
            result = keep.tile([P, g1 - g0, j1 - j0], F32, name=f"result{g0}_{j0}")
            if on_vector:
                nc.vector.tensor_copy(result[:], sums[:])
            else:
                nc.scalar.copy(result[:], sums[:])
            nc.sync.dma_start(out_rows[:, g0:g1, j0:j1], result[:])

        roots = {(0, 0): keep.tile([P, PACK, S], F32, name="root0")}
        for c0 in (0, BANK):
            roots[1, c0] = keep.tile([P, PACK, BANK], F32, name=f"root1_{c0}")
        unit = [[[(b, t, 0, BANK)], [(b, t, BANK, S)]] for b in range(2) for t in range(PACK)][:6]
        unit[0] = [[(0, 0, j0, j0 + 256)] for j0 in range(0, S, 256)]
        last = len(unit) - 1
        late = [(2, 0), (3, 0), (3, BANK), (2, BANK)]
        late_tiles = [diffs[0], keep.tile([P, S], F32, name="diff_late")]
        late_diff = [late_tiles[i // 2][:, i % 2 * BANK : (i % 2 + 1) * BANK] for i in range(4)]
        opened, h_bf, banks = {}, {}, {}

        def interleave(b, j0, split, slot, width=BANK):
            base = j0 // BANK * BANK * b
            h_bf[b, j0] = square_and_interleave(staged[slot], roots[b, base], j0 - base, width, split)

        def quantize(b, j0, width=BANK):
            quantize_h(b, j0, j0 + width, h_bf[b, j0])

        def open_chunk(j0, width=BANK):
            groups = BANK // width
            opened[j0] = [open_sums(g, g + groups, j0, j0 + width) for g in range(0, N // P, groups)]

        def finish_chunk(j0, first, on_vector):
            for sums, v in zip(opened[j0][first:], on_vector):
                finish(sums, v)

        def project_late(i):
            t, j0 = late[i]
            banks[i] = project([(1, t, j0, j0 + BANK)])

        def gather_late(i, c0=0, c1=BANK):
            t, j0 = late[i]
            nc.vector.tensor_copy(copies[i % 2][:, c0:c1], ref[1][t][:].indirect(offsets[:, (j0 + c0) // GROUP : (j0 + c1) // GROUP]))

        def subtract_late(i, c0=0, c1=BANK):
            nc.vector.tensor_tensor(late_diff[i][:, c0:c1], banks[i][:, c0:c1], copies[i % 2][:, c0:c1], ALU.subtract)

        def root_late(i, squares, c0=0, c1=BANK):
            t, j0 = late[i]
            per_row = inv_gain[:, 1, t : t + 1]
            nc.scalar.activation(roots[1, j0][:, t, c0:c1], squares[:, c0:c1], ACT.Abs_reciprocal_sqrt, bias=per_row, scale=per_row)

        def square_on_gpsimd(part):
            nc.gpsimd.tensor_tensor(part, part, part, ALU.mult)

        latent(0)
        latent(1)
        for u in range(len(unit)):
            difference(u, merge=u > 0)
            if u in (1, 2):
                cast_and_quantize_w1(1, u - 1)
            if u == last:
                inverse_roots(u - 1, 1, (0,))
            elif u > 0:
                inverse_roots(u - 1, 2 if u in (1, 4) else 1)
            if u == last:
                interleave(0, 0, BANK, 0)
            if u + 2 <= last:
                latent(u + 2)
            else:
                project_late(2 * (u + 1 - last))
                project_late(2 * (u + 1 - last) + 1)
            if u == last - 1:
                nc.scalar.activation(diffs[u % 3][:, :BANK], diffs[u % 3][:, :BANK], ACT.Square)
            elif u < last:
                square(u, False, 2 if u in (0, 3) else 1)
        spare = diffs[last % len(diffs)]
        held = diffs[(last - 1) % len(diffs)][:, BANK:]
        nc.gpsimd.tensor_tensor(copies[2][:, BANK:], held, held, ALU.mult)
        square_on_gpsimd(spare[:, :BANK])
        square_on_gpsimd(spare[:, BANK:])
        gather_late(0)
        subtract_late(0)
        square_on_gpsimd(late_diff[0])
        nc.scalar.activation(roots[1, BANK][:, 0, :], copies[2][:, BANK:], ACT.Abs_reciprocal_sqrt, bias=inv_gain[:, 1, 0:1], scale=inv_gain[:, 1, 0:1])
        inverse_roots(last)
        interleave(0, BANK, BANK, 1)
        gather_late(1)
        subtract_late(1)
        gather_late(2)
        subtract_late(2)
        quantize(0, 0)
        open_chunk(0)
        square_on_gpsimd(late_diff[2])
        gather_late(3)
        subtract_late(3)
        nc.scalar.activation(spare[:, BANK:], late_diff[1], ACT.Square)
        root_late(0, late_diff[0])
        root_late(1, spare[:, BANK:])
        interleave(1, 0, 320, 0)
        quantize(1, 0)
        quantize(0, BANK)
        open_chunk(BANK, HALF)
        open_chunk(BANK + HALF, HALF)
        root_late(2, late_diff[2])
        nc.vector.tensor_tensor(late_diff[3], late_diff[3], late_diff[3], ALU.mult)
        root_late(3, late_diff[3])
        finish_chunk(0, 0, (True,))
        interleave(1, BANK, 192, 2, HALF)
        quantize(1, BANK, HALF)
        interleave(1, BANK + HALF, 192, 1, HALF)
        quantize(1, BANK + HALF, HALF)
        finish_chunk(0, len((True,)), (False, False, False))
        finish_chunk(BANK, 0, (True, False))
        finish_chunk(BANK + HALF, 0, (True, False))
